import numpy as np, ml_dtypes
CORES = [13,21,141,149]
N = 4
BF = ml_dtypes.bfloat16
V, P, L, RO, Q, CAP = 1280, 2048, 256, 3, 3, 96
H, ST = 1024, 5
MS, PO = (4, 4, 5, 5, 6, 6, 7, 8), 14
def rings(rng, hole):
    pool = 1 + np.argsort(rng.random((8, 16, 255)), axis=-1)[..., :PO]
    ms = np.stack([rng.permutation(np.array(MS)) for r in range(N)])
    pal = np.take_along_axis(np.broadcast_to(pool, (N, 8, 16, PO)), np.argsort(rng.random((N, 8, 16, PO)), axis=-1), 3)
    k = np.take_along_axis(pal, (rng.random((N, 8, 16, V)) * ms[:, :, None, None]).astype(np.int64), 3)
    u = rng.random((N, 8, 16, V))
    return np.where(u < hole, 0, np.where(u < hole + 0.05, rng.integers(1, 256, (N, 8, 16, V)), k))
def parts(rng, hole=0.12):
    t = rng.choice(np.array([0, 300, 500, 700, 850]), (N, 8, 16, 1)) + rng.integers(0, 100, (N, 8, 16, 1))
    return rings(rng, hole), rng.integers(0, V, (N, 8, 16, V)), rng.integers(0, 256, (N, 8, 16, P)), rng.integers(0, 256, (N, 8, 16, L)), t
def pack(k, b, x, z, t):
    def bf(a): return np.ascontiguousarray(a.reshape(N, 128, -1)).astype(np.float32).astype(BF)
    return {"ring": bf(k), "nbr": np.ascontiguousarray(b.reshape(N, 128, V)).astype(np.int32), "mat": bf(x), "z0": bf(z), "thr": np.ascontiguousarray(t.reshape(N, 128, 1)).astype(np.int32)}
def setup_inputs(rng):
    return pack(*parts(rng))
def setup_inputs_spread(rng):
    k, b, x, z, t = parts(rng)
    e = rng.integers(5, 13, (N, 8, 1, 1)); ix = np.minimum((255 * rng.random((N, 8, 16, V)) ** e).astype(np.int64), 254)
    keys = 1 + np.argsort(rng.random((8, 16, 255)), axis=-1)
    k = np.take_along_axis(np.broadcast_to(keys, (N, 8, 16, 255)), ix, 3)
    k = np.where(rng.random((N, 8, 16, V)) < rng.random((N, 8, 1, V)) ** 3, 0, k)
    b[:, ::2] = np.minimum((V * rng.random((N, 4, 16, V)) ** 2).astype(np.int64), V - 1)
    x = np.minimum((np.exp2(8 * rng.random((N, 8, 1, P))) * rng.random((N, 8, 16, P))).astype(np.int64), 255)
    z = np.minimum((np.exp2(8 * rng.random((N, 8, 1, L))) * rng.random((N, 8, 16, L))).astype(np.int64), 255)
    t = np.minimum(np.exp2(12 * rng.random((N, 8, 16, 1))).astype(np.int64), 4095)
    return pack(k, b, x, z, t)
def setup_inputs_ends(rng):
    k, b, x, z, t = parts(rng)
    c = rng.random((N, 8, 1, V)); dens = rng.choice(np.array([0.25, 0.25, 0.5]), (N, 8, 1, V))
    k = np.where(c < 0.25, 255, np.where(c < 0.4, 0, np.where(c < 0.85, 255 * (rng.random((N, 8, 16, V)) < dens), k)))
    k[:, 6, :, 2 * ST:ST * (L - 4):ST] = 255
    b = np.where(rng.random((N, 8, 16, V)) < 0.7, (V - 1) * rng.integers(0, 2, (N, 8, 16, V)), b)
    share = np.array([0.5, 0, 0.5, 0, 0, 0, 0, 0]).reshape(8, 1, 1)
    x = np.where(rng.random((N, 8, 1, P)) < share + 0.05, 255 * rng.integers(0, 2, (N, 8, 1, P)), 255 * rng.integers(0, 2, (N, 8, 16, P)))
    z = np.where(rng.random((N, 8, 1, L)) < share, 255 * rng.integers(0, 2, (N, 8, 1, L)), 255 * rng.integers(0, 2, (N, 8, 16, L)))
    t = np.broadcast_to(4095 * (rng.random((1, 8, 16, 1)) < 0.25), (N, 8, 16, 1)); t = np.where(rng.random((N, 8, 16, 1)) < 0.05, 4095 - t, t)
    t[:, 0, 0] = 4095; t[:, 7, 14] = 0; t[:, 7, 15] = 4095
    k[..., V - 1] = 255; k[..., 0] = 255 * (np.argsort(np.argsort(rng.random((N, 8, 16)), axis=-1), axis=-1) < 5)
    x[..., 0] = 0; x[..., P - 1] = 255
    p = np.arange(16)
    for lane in (1, L - 1):
        v = ST * lane; z[..., lane] = 255; k[..., v] = 0; b[:, :, 0, v] = V - 1
        x[..., ((255 * (2 * v + 1) >> 2) + 811 * p) & (P - 1)] = 0 if lane == 1 else 255 * ((p + 1) & 1)
    z[..., 0] = 0; z[..., L - 2] = 0; k[..., ST * (L - 2)] = 0
    a = (15 + Q) >> 1; v = ST * (L - 4); z[..., L - 4] = 0
    k[..., v] = 255 * (p < a); k[..., V - 2] = 255 * (p >= 16 - a); b[:, :, 0, v] = V - 2
    k[..., V - 3] = 255; k[..., V - 4] = 255; b[:, :, 0, V - 2] = V - 2
    for i, u in ((1, V - 1), (14, V - 3), (15, V - 4)): b[:, :, i, V - 2] = u
    return pack(k, b, x, z, t)
def setup_inputs_corners(rng):
    k, b, x, z, t = parts(rng)
    code = rng.integers(1, 256, (N, 8, 16, 1)); code[:, ::2] = code[:1, ::2]; row = np.arange(16)[:, None]
    u = rng.random((N, 8, 1, V))
    k = np.where((row < Q) | (u < 0.33), code, np.where(u < 0.66, rng.integers(1, 256, (N, 8, 16, V)), 0))
    own = np.broadcast_to(np.arange(V), (16, V)); many = (0, 1, CAP - 1, CAP, CAP + 1, L, CAP, L >> 1)
    for r in range(N):
        for g in range(8):
            n = many[(g + r) & 7]; lanes = rng.permutation(L)[:n]; vf = ST * lanes
            if g & 3 == 1: b[r, g] = np.where(rng.random((16, V)) < 0.5, own, b[r, g])
            if g & 3 == 2: b[r, g] = np.where(rng.random((16, V)) < 0.3, (V - 1) * rng.integers(0, 2, (16, V)), b[r, g])
            if g & 3 == 3: b[r, g] = np.where(rng.random((16, V)) < 0.5, rng.integers(0, V, (1, V)), b[r, g])
            gone = np.zeros(V, bool); gone[vf] = True
            b[r, g] = b[r, g] + gone[b[r, g]]
            if g & 3 == 1: b[r, g][:, vf[::2]] = vf[::2]
            k[r, g][:, vf] = np.where((row < Q - 1) & (rng.random(n) < 0.5), code[r, g], 0)
    t = np.where(rng.random((N, 8, 16, 1)) < 0.5, rng.choice(np.array([0, 1, 15, 600, 1000, 4095]), (N, 8, 16, 1)), t); t[:, ::2, :Q] = 0; t[:, 1, 15] = 4095
    x = np.where(rng.random((N, 8, 1, P)) < 0.2, rng.choice(np.array([0, 128, 255]), (N, 8, 1, P)), x)
    z = np.where(rng.random((N, 8, 1, L)) < 0.3, rng.choice(np.array([0, 1, 254, 255]), (N, 8, 1, L)), z)
    return pack(k, b, x, z, t)
def setup_inputs_crowd(rng):
    k, b, x, z, t = parts(rng, 0.22)
    k = np.where(rng.random((N, 8, 1, V)) < 0.03, 0, k)
    hubs = np.argsort(rng.random((N, 8, V)), axis=-1)[..., :12]
    h = np.take_along_axis(hubs, rng.integers(0, 12, (N, 8, 16 * V)), 2).reshape(N, 8, 16, V)
    b = np.where(rng.random((N, 8, 16, V)) < 0.6, h, b)
    x[:, 1::2] = np.take_along_axis(x[:, 1::2], np.broadcast_to(rng.integers(0, 8, (N, 4, 1, P)), (N, 4, 16, P)), 3)
    z[..., 1::2] = z[..., ::2]
    return pack(k, b, x, z, t)
def setup_inputs_far(rng):
    k, b, x, z, t = parts(rng); a = (15 + Q) >> 1; kk = np.arange(16)[:, None]
    up = rng.integers(0, 2, (N, 8, 1, 1)); up[0, 0] = 0; up[N - 1, 7] = 1
    x = rng.integers(0, 48, (N, 8, 16, P)) + 208 * up; z = rng.integers(0, 48, (N, 8, 16, L)) + 208 * (1 - up)
    t = np.where(rng.random((N, 8, 16, 1)) < 0.4, rng.integers(3000, 3500, (N, 8, 16, 1)), t)
    first = ST * np.arange(L); rest = np.setdiff1d(np.arange(V), first)
    for r in range(N):
        for g in range(8):
            if (g + r) & 1: continue
            code = rng.integers(1, 256, (16, 1)); o = rng.permutation(16)[:, None]
            rare = 1 + (code - 1 + rng.integers(1, 255, (16, V))) % 255
            other = np.where(rng.random((16, V)) < 0.7, 0, rare)
            u = rng.permutation(rest); q = len(u) >> 2; near = u[:q]; full = u[q:2 * q]; right = u[2 * q:3 * q]
            kr = k[r, g]; br = b[r, g]
            kr[:, first] = np.where(o < a, code, other[:, first])
            kr[:, right] = np.where(o >= 16 - a, code, other[:, right])
            kr[:, full] = code
            kr[:, near] = np.where(o == rng.integers(a, 16, q), rare[:, near], code)
            e = ST * rng.permutation(L)[:L >> 4]
            kr[:, e[::2]] = 0; kr[:, e[1::2]] = code
            br[:, first] = rng.choice(right, (16, L))
            i = rng.integers(0, 15, q); m = i + 1 + (rng.random(q) * (15 - i)).astype(np.int64)
            pick = rng.random((16, q)); low = rng.choice(near, (16, q)); top = rng.choice(full, (16, q)); poor = rng.choice(np.concatenate([first, u[2 * q:]]), (16, q))
            late = np.where((kk == m) | (pick < 0.4), top, np.where(pick < 0.7, low, poor))
            early = np.where((kk == i) | ((kk > i) & (pick < 0.5)), low, poor)
            br[:, right] = np.where(kk < m, early, late)
    return pack(k, b, x, z, t)
def check_inputs(d):
    bad = []
    for k, lo, hi in (("ring", 0, 255), ("nbr", 0, V - 1), ("mat", 0, 255), ("z0", 0, 255), ("thr", 0, 4095)):
        a = np.asarray(d[k]).astype(np.float64)
        if not (np.min(a) >= lo and np.max(a) <= hi): bad.append("range of " + k)
        elif np.any(a != np.floor(a)): bad.append("whole numbers in " + k)
    return bad
def columns(a, ix):
    return np.take_along_axis(a, ix[:, :, None, :], 3)
def by_lane(a):
    return np.ascontiguousarray(a.transpose(0, 1, 3, 2)).reshape(N, 8, L * 16)
def reference(ring, nbr, mat, z0, thr):
    K = ring.astype(np.float32).astype(np.int64).reshape(N, 8, 16, V); B = nbr.astype(np.int64).reshape(N, 8, 16, V)
    X = mat.astype(np.float32).astype(np.int64).reshape(N, 8, 16, P); z = z0.astype(np.float32).astype(np.int64).reshape(N, 8, 16, L)
    th = thr.astype(np.int64).reshape(N, 8, 16, 1); v = np.array(np.broadcast_to(ST * np.arange(L), (N, 8, L)))
    failures = np.zeros(N, np.int64); rv_old = np.zeros((N, 8, 16), np.int64); row = np.arange(16)[:, None]
    for t in range(RO):
        j = (np.sum(z, axis=2) + t) & 15
        n = np.take_along_axis(columns(B, v), j[:, :, None, :], 2)[:, :, 0]
        Kv = columns(K, v); Kn = columns(K, n)
        direct = np.sum((Kv == Kn) & (Kv > 0), axis=2) >= Q
        cand = by_lane(columns(B, n)); Kc = columns(K, cand).reshape(N, 8, 16, L, 16)
        score = np.minimum(np.sum((Kc == Kv[..., None]) & (Kc > 0), axis=2), np.sum((Kc == Kn[..., None]) & (Kc > 0), axis=2))
        k = np.argmax(score, axis=3)
        bridged = ~direct & (np.max(score, axis=3) >= Q); failed = ~direct & ~bridged
        w = np.where(bridged, np.take_along_axis(cand.reshape(N, 8, L, 16), k[..., None], 3)[..., 0], n)
        Kw = columns(K, w)
        place = (((Kw * (2 * v + 1)[:, :, None, :]) >> 2) + 811 * row + t) & (P - 1)
        Xc = columns(X, by_lane(place)).reshape(N, 8, 16, L, 16)
        d = np.sum(np.abs(Xc - z[..., None]), axis=2)
        p = np.argmin(d, axis=3)
        x = np.take_along_axis(Xc, p[:, :, None, :, None], 4)[..., 0]
        caught = (d.transpose(0, 1, 3, 2) < th + (failures & 15)[:, None, None, None]) & (Kw > 0)
        low = np.argmax(caught, axis=3)
        rv = np.where(np.any(caught, axis=3), np.take_along_axis(Kw, low[..., None], 3)[..., 0], 0)
        fi = failed.astype(np.int64); served = failed & (np.add.accumulate(fi, axis=2) - fi < CAP)
        h = np.sum(Kw * z, axis=2) & (H - 1)
        given = columns(np.roll(K, -1, axis=0), h)
        filled = np.where(Kv > 0, Kv, np.where(bridged[:, :, None, :], Kw, given))
        K2 = np.array(K); B2 = np.array(B); active = bridged | served
        for a in range(N):
            for g in range(8):
                i = np.nonzero(active[a, g])[0]
                u, first = np.unique(v[a, g, i], return_index=True); i = i[first]
                K2[a, g][:, u] = filled[a, g][:, i]
                i = i[bridged[a, g, i]]; B2[a, g, j[a, g, i], v[a, g, i]] = w[a, g, i]
        come = np.roll(rv_old, 1, axis=0)
        K = np.where((K2 == rv[..., None]) | (K2 == come[..., None]), 0, K2); B = B2
        z = (z + x) >> 1; v = w; rv_old = rv; failures = np.sum(fi, axis=(1, 2))
    return {"yk": K.reshape(N, 128, V).astype(np.float32).astype(BF), "yz": z.reshape(N, 128, L).astype(np.float32)}

@@ -1,0 +1,768 @@
+from concourse.bass import DstId, RemoteDMATransfer
+from concourse.mybir import dt, AluOpType, AxisListType, ActivationFunctionType
+import comms_topo
+
+A = AluOpType
+AF = ActivationFunctionType
+RO, SB, CAP = 3, 2048, 96
+BIG = 1.0e9
+PEQ = (0, 2)
+REM = 1536
+WS = 17 * SB
+DIR = 239 * SB
+
+F32 = dict(If=128, G16f=128, G8f=8, DM=256, RN=256, RP=128, T1=1280, B=1536, Bv=256, mB=256, Bk=256, dg=256, sc=256, BnC=256,
+           dr=16, kn=16, cV=256, mn=256, sc2=256, W=16, Aw=256, kp=256, Vn=256, V2=256, pr=256, zx=256, sd=256,
+           Ap=256, dk=256, cd=256, rr=256, ohw=256, zF=256, pcol=1, p2=1, p2b=1, dcol=1, odd=1, even=1, kcol=1, thr=1, thrc=1,
+           nrv=1, rvE0=1, rvE1=1, rvE2=1, ga=1, gb=1, gr=1, gc=1, rvm=1, ncome=1, fs=1, fj=16, d04=16, vmd4=16, x96=16, y96=16,
+           wr=16, wr2=16, ha=16, hb=16, hc=16, src=16, w2=16, word=16, t1=16, Aq=256, pm0=1, pm1=1, pm2=1, pl0=1, pl1=1, pl2=1,
+           p5=1, fb=1)
+BF = dict(Ib=128, G16b=128, G8b=8, G8s=8, G8k=8, TriO=128, On=128, LPh=128, LPl=128, UC=256, z=256, Kv=256, Kn=256,
+          Kw=256, evn=256, m0=256, m1=256, Kvr=256, zT=256, hz=256, hole=256, fm=256, code=256, cdE=256, cdO=256, F=16, Lb=16,
+          act=16, NM1=1280, NM2=1280)
+I32 = dict(PI=1, pi15=1, pb=1, D1=256, D15=256, D2=128, D3=256, ic=16, iv=16, y1=256, y2=256, wi=16, wi2=16, pl=256, plm=256,
+           pi=16, pi2=16, dz=256, Wi=16, wT=16, hi=16, h2=16, qi=16, q1=16, q2=16, rvi=1, rva=1, fi=1, fa=1, ci=256, cb=256)
+U16 = dict(bl=16, bl2=16, vO=32, nO=32, wO=32, scO=16, srO=16, dO=32, BnL=256, PL=256)
+
+
+def _layout(d):
+    pos, at = {}, 0
+    for n in d:
+        pos[n] = at
+        at += (d[n] + 15) // 16 * 16
+    return pos, at
+
+
+_PF, _NF = _layout(F32)
+_PB, _NB = _layout(BF)
+_PI, _NI = _layout(I32)
+_PU, _NU = _layout(U16)
+WHERE = {}
+for _d, _p, _n in ((F32, _PF, "SF"), (BF, _PB, "SBF"), (I32, _PI, "SI"), (U16, _PU, "SU")):
+    for _k in _d:
+        WHERE[_k] = (_n, _p[_k], _d[_k])
+_BIGB = dict(KK0=(REM + 1024 * RO, "bfloat16"), KK1=(REM + 1024 * RO, "bfloat16"), RS=(2048, "bfloat16"), X=(2048, "bfloat16"),
+             Kc=(4096, "bfloat16"), eqV=(4096, "bfloat16"), eqN=(4096, "bfloat16"), Xc=(4096, "bfloat16"), df=(4096, "bfloat16"),
+             ab=(4096, "bfloat16"), EA=(2048, "bfloat16"), EB=(1024, "bfloat16"), E0=(2048, "bfloat16"), E1=(1024, "bfloat16"),
+             NBi=(1280, "int32"), Yk=(1280, "bfloat16"), thI=(8, "int32"), rS0=(8, "float32"), rS1=(8, "float32"),
+             rS2=(8, "float32"), cI0=(8, "float32"), cI1=(8, "float32"))
+SCRATCH = {"SF": ("sbuf", [128, _NF], "float32"), "SBF": ("sbuf", [128, _NB], "bfloat16"), "SI": ("sbuf", [128, _NI], "int32"),
+           "SU": ("sbuf", [128, _NU], "uint16")}
+for _k in _BIGB:
+    SCRATCH[_k] = ("sbuf", [128, _BIGB[_k][0]], _BIGB[_k][1])
+    WHERE[_k] = (_k, 0, _BIGB[_k][0])
+for _k in range(8):
+    SCRATCH["b%d" % _k] = ("psum", [128, 512], "float32")
+    WHERE["b%d" % _k] = ("b%d" % _k, 0, 512)
+for _k in range(RO):
+    SCRATCH["hand%d" % _k] = ("sbuf", [128, 512], "bfloat16")
+for _k in range(RO - 1):
+    SCRATCH["hrv%d" % _k] = ("sbuf", [128, 8], "float32")
+SEMAPHORES = ["qv", "qs", "qt", "qg"]
+SEMAPHORES += ["ld%d" % i for i in range(8)] + ["st%d" % i for i in range(5)]
+for _t in range(RO):
+    SEMAPHORES += ["ks%d0" % _t, "ks%d1" % _t, "ki%d0" % _t, "ki%d1" % _t, "ha%d" % _t, "hs%d" % _t]
+for _t in range(RO - 1):
+    SEMAPHORES += ["rs%d" % _t, "ri%d" % _t, "ra%d" % _t, "rl%d" % _t]
+
+CY = 0.00083
+SEQ = []
+
+
+def relays(core, T, topo, dst):
+    out = []
+    for d in (topo.die(core), 1 - topo.die(core)):
+        for c in topo.cores_of(core):
+            if c != core and topo.die(c) == d and T.rank_of(c) is None and topo.may_write(c, dst):
+                out.append(c)
+                break
+    return out
+
+
+def engines_mask(topo, src, dst, n):
+    m = 0
+    for e in topo.engines(src, dst)[:n]:
+        m |= 1 << e
+    return m
+
+
+def remote(g, topo, src, dst, out, in_, rsem, lsem, n):
+    rid, pid = topo.addr(dst, src)
+    return g.remote_dma(out, in_, rsem, lsem, pid, rid, engines_mask(topo, src, dst, n))
+
+
+def view(name, lo=0, hi=None, step=1, plo=0, phi=128):
+    return ("@", name, lo, WHERE[name][2] if hi is None else hi, step, plo, phi)
+
+
+def ind(win, off):
+    return ("#", win, off)
+
+
+def is_view(x):
+    return isinstance(x, tuple) and len(x) > 0 and (x[0] == "@" or x[0] == "#")
+
+
+def count(x):
+    if x[0] == "#":
+        return 16 * (x[2][3] - x[2][2])
+    return (x[3] - x[2] + x[4] - 1) // x[4]
+
+
+def psum(x):
+    return x[0] == "@" and x[1][0] == "b" and len(x[1]) == 2 and x[1][1].isdigit()
+
+
+def two(x):
+    return x[0] == "@" and WHERE[x[1]][0] not in ("SF", "SI", "NBi", "thI") and not psum(x)
+
+
+def clash(a, b):
+    if a[3] <= b[2] or b[3] <= a[2] or a[6] <= b[5] or b[6] <= a[5]:
+        return False
+    if a[4] > 1 and a[4] == b[4] and (a[2] - b[2]) % a[4]:
+        return False
+    return True
+
+
+def covers(a, b):
+    return a[4] == 1 and a[2] <= b[2] and a[3] >= b[3] and a[5] <= b[5] and a[6] >= b[6]
+
+
+def cost(q, m, kw):
+    o = kw.get("out")
+    if q == "t":
+        n, mm = count(kw["rhs"]), count(kw["lhsT"])
+        f = 4 if WHERE[kw["lhsT"][1]][0] == "SF" else 1
+        return max(min(64, mm), n) * f * CY
+    if q == "g":
+        return 0.15 + 2 * count(o) * CY
+    ins = [kw[k] for k in kw if k not in ("out", "accum_out") and is_view(kw[k])]
+    full = [i for i in ins if count(i) > 1]
+    n = max([count(o)] + [count(i) for i in full])
+    if o[0] == "#":
+        return 0.05 + n * 3.8 * CY
+    for i in full:
+        if i[0] == "#":
+            return 0.06 + n * 1.56 * CY
+    c = 1.0
+    if q == "v" and m == "tensor_tensor" and not psum(o) and not [i for i in full if psum(i)]:
+        c = 2.0
+    if q == "v" and m in ("tensor_copy", "tensor_scalar", "memset") and two(o) and not [i for i in full if not two(i)]:
+        c = 0.5
+    return max(64, n * c) * CY
+
+
+def noter(T):
+    ops, hist, opened = [], {}, {}
+
+    def res(x):
+        if x[0] == "#":
+            return res(x[1]).indirect(res(x[2]))
+        b, off, _ = WHERE[x[1]]
+        lo, hi = off + x[2], off + x[3]
+        if x[4] > 1:
+            return T[b][x[5]:x[6], lo:range(lo, hi, x[4])[-1] + 1:x[4]]
+        return T[b][x[5]:x[6], lo:hi]
+
+    def touch(i, q, v, wr, deps):
+        ps = psum(v)
+        keep = []
+        for e in hist.setdefault(v[1], []):
+            ev, ew, eq, ei = e
+            if ei == i:
+                keep.append(e)
+                continue
+            if ps and eq != q:
+                deps.add((ei, True))
+                if wr and covers(v, ev):
+                    continue
+            elif (wr or ew) and clash(v, ev):
+                if not (ps and q == "t"):
+                    deps.add((ei, True))
+                if wr and covers(v, ev):
+                    continue
+            keep.append(e)
+        keep.append((v, wr, q, i))
+        hist[v[1]] = keep
+
+    def rec(q, c, tail, reads, writes, emit, sem=None, inc=1):
+        i = len(ops)
+        deps = set()
+        for v in reads:
+            touch(i, q, v, False, deps)
+        for v in writes:
+            touch(i, q, v, True, deps)
+        ops.append([q, c, tail, deps, emit, sem or "q" + q, inc])
+        return i
+
+    def op(q, m, **kw):
+        reads, writes = [], []
+        for k in kw:
+            x = kw[k]
+            if not is_view(x):
+                continue
+            w = k in ("out", "accum_out")
+            if x[0] == "#":
+                (writes if w else reads).append(x[1])
+                reads.append(x[2])
+            else:
+                (writes if w else reads).append(x)
+
+        def emit(e):
+            a = {}
+            for k in kw:
+                a[k] = res(kw[k]) if is_view(kw[k]) else kw[k]
+            if m == "memset":
+                return e.memset(a["out"], a["constant"])
+            if m == "tensor_copy":
+                return e.tensor_copy(a["out"], a["in_"])
+            if m == "tensor_tensor":
+                return e.tensor_tensor(**a)
+            if m == "tensor_scalar":
+                return e.tensor_scalar(**a)
+            if m == "tensor_reduce":
+                return e.tensor_reduce(**a)
+            if m == "tensor_tensor_scan":
+                return e.tensor_tensor_scan(**a)
+            if m == "matmul":
+                return e.matmul(**a)
+            if m == "activation":
+                return e.activation(**a)
+            if m == "affine_select":
+                return e.affine_select(**a)
+            return e.iota(**a)
+        i = rec(q, cost(q, m, kw), 0.06, reads, writes, emit)
+        if m == "matmul":
+            b = kw["out"][1]
+            if b in opened:
+                for j in (opened[b] if kw["start"] or kw["stop"] else opened[b][:1]):
+                    ops[i][3].add((j, False))
+            if kw["start"] or kw["stop"]:
+                opened[b] = [i]
+            else:
+                opened[b].append(i)
+        return i
+
+    def land(v, sem, inc, i):
+        j = rec("x", 0.0, 8.0, [], [v], None, sem, inc)
+        ops[j][3].add((i, True))
+
+    return ops, op, rec, land, res
+
+
+def order(ops):
+    n = len(ops)
+    users = [[] for _ in range(n)]
+    left = [0] * n
+    for i in range(n):
+        for j, w in ops[i][3]:
+            users[j].append((i, w))
+            left[i] += 1
+    prio = [0.0] * n
+    for i in range(n - 1, -1, -1):
+        b = 0.0
+        for u, w in users[i]:
+            b = max(b, prio[u] + (ops[i][2] if w else 0.0))
+        prio[i] = b + ops[i][1]
+    ready = [0.0] * n
+    avail = {}
+    free = {}
+    for i in range(n):
+        if left[i] == 0:
+            avail.setdefault(ops[i][0], []).append(i)
+    out = []
+    while len(out) < n:
+        best = None
+        for q in avail:
+            if not avail[q]:
+                continue
+            f = free.get(q, 0.0)
+            s0 = min(max(f, ready[i]) for i in avail[q])
+            i = max((i for i in avail[q] if max(f, ready[i]) <= s0 + 0.03), key=lambda k: (prio[k], -k))
+            s = max(f, ready[i])
+            if best is None or s < best[0]:
+                best = (s, q, i)
+        s, q, i = best
+        avail[q].remove(i)
+        free[q] = s + ops[i][1] if q != "x" else 0.0
+        out.append(i)
+        for u, w in users[i]:
+            ready[u] = max(ready[u], s + (ops[i][1] + ops[i][2] if w else 0.0))
+            left[u] -= 1
+            if left[u] == 0:
+                avail.setdefault(ops[u][0], []).append(u)
+    return out
+
+
+def issue(g, T, ops, seq):
+    Q = {"v": g.vector, "s": g.scalar, "t": g.tensor, "g": g, "y": g.sync, "S": g.scalar}
+    total, tok, know = {}, {}, {}
+    for q in Q:
+        know[q] = {}
+    know["S"] = know["s"]
+    for i in seq:
+        q, c, tail, deps, emit, sem, inc = ops[i]
+        if emit is None:
+            total[sem] = total.get(sem, 0) + inc
+            tok[i] = (sem, total[sem], {})
+            continue
+        k = know[q]
+        need = {}
+        for j, w in deps:
+            if w:
+                s, v, sn = tok[j]
+                if k.get(s, 0) < v and (s not in need or need[s][0] < v):
+                    need[s] = (v, sn)
+        for s in sorted(need):
+            v, sn = need[s]
+            if [o for o in need if o != s and need[o][1].get(s, 0) >= v]:
+                continue
+            Q[q].wait_ge(T.sem[s], v)
+        for s in need:
+            v, sn = need[s]
+            k[s] = max(k.get(s, 0), v)
+            for o in sn:
+                k[o] = max(k.get(o, 0), sn[o])
+        total[sem] = total.get(sem, 0) + inc
+        r = emit(Q[q])
+        if r is not None:
+            r.then_inc(T.sem[sem], inc)
+        tok[i] = (sem, total[sem], dict(k))
+    for s in sorted(total):
+        if know["g"].get(s, 0) < total[s]:
+            g.wait_ge(T.sem[s], total[s])
+
+
+def rank_program(g, core, T, topo):
+    rank = T.rank_of(core)
+    n = len(T.cores)
+    if rank is None:
+        hand_on(g, core, T, topo)
+        return
+    ops, op, rec, land, res = noter(T)
+    below, above = T.cores[(rank - 1) % n], T.cores[(rank + 1) % n]
+    rl = relays(core, T, topo, below)
+    rv_relay = relays(core, T, topo, above)[0]
+    v = view
+
+    def tt(out, a, b, o):
+        return op("v", "tensor_tensor", out=out, in0=a, in1=b, op=o)
+
+    def ts(out, a, s1, o1, s2=None, o2=None):
+        if o2 is None:
+            return op("v", "tensor_scalar", out=out, in0=a, scalar1=s1, scalar2=None, op0=o1)
+        return op("v", "tensor_scalar", out=out, in0=a, scalar1=s1, scalar2=s2, op0=o1, op1=o2)
+
+    def cp(out, a):
+        return op("v", "tensor_copy", out=out, in_=a)
+
+    def act(out, a, f=AF.Copy, **kw):
+        return op("s", "activation", out=out, in_=a, func=f, **kw)
+
+    def mm(out, l, r, start=True, stop=True):
+        return op("t", "matmul", out=out, lhsT=l, rhs=r, start=start, stop=stop)
+
+    def iota(out, pattern, base, cm):
+        kw = dict(out=out, pattern=pattern, base=base, channel_multiplier=cm)
+        if WHERE[out[1]][0] != "SI":
+            kw["allow_small_or_imprecise_dtypes"] = True
+        return op("g", "iota", **kw)
+
+    def scan(out, a, b, o1):
+        return op("v", "tensor_tensor_scan", out=out, data0=a, data1=b, initial=0.0, op0=A.add, op1=o1)
+
+    def load(q, dst, src, k):
+        return rec(q, 0.1, 4.0, [], [dst], lambda e: e.dma_start(res(dst), src), "ld%d" % k, 16)
+
+    def store(dst, srcv, k):
+        return rec("y", 0.1, 2.0, [srcv], [], lambda e: e.dma_start(dst, res(srcv)), "st%d" % k, 16)
+
+    def hv(name, c, w=128):
+        return v(name, w * c, w * c + w)
+
+    def turn(c):
+        if [q for q in PEQ if q // 2 == c]:
+            mm(v("b7", 0, 128), hv("z", c), v("Ib"))
+            act(hv("zT", c), v("b7", 0, 128), scale=-1.0)
+
+    load("y", v("NBi", 0, 640), T.nbr[:, 0:640], 0)
+    load("S", v("z"), T.z0[:], 1)
+    load("S", v("NBi", 640, 1280), T.nbr[:, 640:1280], 2)
+    load("y", v("KK0", 0, 1280), T.ring[:], 3)
+    load("S", v("thI", 0, 1), T.thr[:], 4)
+    load("y", v("X"), T.mat[:], 5)
+
+    iota(v("PI"), [[1, 1]], 0, 1)
+    iota(v("D2"), [[-16, 8], [0, 16]], 128, 1)
+    iota(v("D1"), [[-1, 256]], 256, 1)
+    iota(v("iv"), [[80, 16]], 0, 0)
+    iota(v("D3"), [[0, 16], [1, 16]], 0, 0)
+    iota(v("ic"), [[1, 16]], 0, 0)
+    iota(v("V2"), [[10, 256]], 1, 0)
+    iota(v("LPh"), [[0, 128]], 0, 16)
+    iota(v("LPl"), [[0, 8], [1, 16]], 0, 0)
+    iota(v("UC"), [[-256, 256]], 65536, 0)
+    iota(v("t1"), [[128, 2], [0, 8]], 1280, 1)
+    iota(v("w2"), [[512, 2], [0, 8]], -1280, 4)
+    iota(v("T1"), [[1, 1280]], 0, 0)
+    ts(v("pi15"), v("PI"), 15, A.bitwise_and)
+    cp(v("pcol"), v("pi15"))
+    ts(v("p5"), v("pcol"), 5.0, A.mult)
+    ts(v("vO", 0, 16), v("iv"), v("p5"), A.add)
+    ts(v("pm0"), v("pcol"), -1.0, A.mult, 16.0, A.add)
+    ts(v("D2"), v("D2"), 4, A.arith_shift_right)
+    ts(v("G16f"), v("D2"), 8.0, A.is_equal)
+    ts(v("G16b"), v("D2"), 8.0, A.is_equal)
+    cp(v("G8f"), v("G16f", 0, 128, 16))
+    cp(v("G8b"), v("G16f", 0, 128, 16))
+    ts(v("G8s"), v("G16f", 0, 128, 16), float(WS), A.mult)
+    ts(v("G8k"), v("G16f", 0, 128, 16), 4096.0, A.mult)
+    ts(v("D15"), v("D1"), 15, A.bitwise_and)
+    ts(v("DM"), v("D15"), 0.0, A.is_equal)
+    ts(v("RN"), v("D3"), 0.0, A.is_equal, -BIG, A.mult)
+    ts(v("RP"), v("RN", 0, 128), -1.0, A.mult)
+    ts(v("If"), v("D1", 0, 128), 256.0, A.is_equal)
+    ts(v("Ib"), v("D1", 0, 128), 256.0, A.is_equal)
+    ts(v("kcol"), v("pcol"), -float(SB), A.mult, -35.0 * SB, A.add)
+    cp(v("bl"), v("ic"))
+    ts(v("bl2"), v("ic"), 16.0, A.mult, 15.0, A.add)
+    for t in range(RO):
+        ts(v("pl%d" % t), v("pcol"), 811.0, A.mult, t - 0.375, A.add)
+        if t:
+            ts(v("pm%d" % t), v("pcol"), -1.0, A.mult, 16.0 + t, A.add)
+    ts(v("TriO"), v("D1", 0, 128), 256.0, A.is_lt)
+    op("v", "memset", out=v("On"), constant=1.0)
+    op("v", "memset", out=v("fb"), constant=-15.0)
+    for i in range(2):
+        op("v", "memset", out=v("KK%d" % i, 1280, REM), constant=0.0)
+    if PEQ:
+        for k in range(16):
+            cp(v("RS", k, 2048, 16), v("Ib"))
+    ts(v("d04"), v("t1"), 8192.0, A.mult)
+    ts(v("vmd4"), v("w2"), 8192.0, A.mult)
+    ts(v("pb"), v("PI"), 4, A.arith_shift_right, 1, A.bitwise_and)
+    cp(v("odd"), v("pb"))
+    ts(v("even"), v("odd"), -1.0, A.mult, 1.0, A.add)
+    for i in range(4):
+        ts(v("pb"), v("PI"), i, A.arith_shift_right, 1, A.bitwise_and)
+        f = 2.0 ** -(2 ** i) - 1.0
+        if i == 0:
+            ts(v("p2"), v("pb"), f, A.mult, 1.0, A.add)
+        else:
+            ts(v("p2b"), v("pb"), f, A.mult, 1.0, A.add)
+            ts(v("p2"), v("p2"), v("p2b"), A.mult)
+    ts(v("dcol"), v("p2"), 0.5, A.mult, -0.5, A.add)
+    cp(v("thr"), v("thI", 0, 1))
+    ts(v("thrc"), v("thr"), float(2 ** 30), A.mult)
+    cp(v("B", 0, 640), v("NBi", 0, 640))
+    cp(v("B", 640, 1280), v("NBi", 640, 1280))
+    for c in range(2):
+        cp(v("b1", 128 * c, 128 * c + 128), hv("z", c))
+        turn(c)
+
+    def send_rings(t):
+        kk = "KK%d" % (t % 2)
+        for h in range(2):
+            src = v(kk, 512 * h, 512 * h + 512)
+
+            def emit(e, h=h, src=src):
+                remote(g, topo, core, rl[h], T["hand%d" % t][:], res(src), T.sem["ha%d" % t], T.sem["ks%d%d" % (t, h)], 8)
+            i = rec("g", 0.3, 4.0, [src], [], emit, "ks%d%d" % (t, h), 8)
+            lo = REM + 1024 * t + 512 * h
+            land(v(kk, lo, lo + 512), "ki%d%d" % (t, h), 8, i)
+
+    def send_revoked(t):
+        src = v("rS%d" % t, 0, 1)
+
+        def emit(e):
+            remote(g, topo, core, rv_relay, T["hrv%d" % t][:, 0:1], res(src), T.sem["ra%d" % t], T.sem["rs%d" % t], 8)
+        i = rec("g", 0.3, 4.0, [src], [], emit, "rs%d" % t, 8)
+        land(v("cI%d" % t, 0, 1), "ri%d" % t, 8, i)
+
+    def K(t):
+        return v("KK%d" % (t % 2), 0, 1280)
+
+    def vo(t, c):
+        b = 16 * (t % 2)
+        return v("vO", b + 8 * c, b + 8 * c + 8)
+
+    def first(t, c):
+        act(hv("Bv", c), ind(v("B", 0, 1280), vo(t, c)))
+        mm(v("b6", 0, 128), v("G16b"), hv("z", c))
+        ts(hv("y1", c), v("b6", 0, 128), v("pm%d" % t), A.add)
+        ts(hv("y2", c), hv("y1", c), 15, A.bitwise_and)
+        oh = v("b1", 256 + 128 * c, 384 + 128 * c)
+        ts(oh, hv("y2", c), 0.0, A.is_equal)
+        tt(hv("mB", c), oh, hv("Bv", c), A.mult)
+        nr = v("b6", 128 + 128 * c, 256 + 128 * c)
+        mm(nr, v("G16f"), hv("mB", c))
+        mm(v("b6", 384 + 8 * c, 392 + 8 * c), hv("mB", c), v("G8f"))
+        tt(hv("dg", c), nr, hv("DM", c), A.mult)
+        scan(hv("sc", c), hv("RN", c), hv("dg", c), A.max)
+        cp(v("nO", 16 * c, 16 * c + 8), v("sc", 128 * c + 15, 128 * c + 128, 16))
+        cp(hv("BnL", c), ind(v("B", 0, 1280), v("nO", 16 * c, 16 * c + 8)))
+        ts(hv("BnC", c), hv("BnL", c), v("kcol"), A.add)
+        if t < RO - 1:
+            tt(hv("Bk", c), hv("Bv", c), hv("mB", c), A.subtract)
+
+    def second(t, c):
+        kv, kn = v("b0", 128 * c, 128 * c + 128), v("b0", 256 + 128 * c, 384 + 128 * c)
+        old = K(max(t - 1, 0))
+        act(hv("Kv", c), ind(old, vo(t, c)))
+        act(hv("Kn", c), ind(old, v("nO", 16 * c, 16 * c + 8)))
+        for raw, dst in (("Kv", kv), ("Kn", kn)):
+            if raw == "Kv":
+                ts(dst, hv(raw, c), 0.0, A.is_equal, -1.0, A.mult)
+                tt(dst, dst, hv(raw, c), A.add)
+            else:
+                ts(dst, hv(raw, c), 0.25, A.max)
+            for i, col, neg in ((0, "cI%d" % (t - 2), "gc"), (1, "rvE%d" % (t - 1), "gr")):
+                if t - 2 + i >= 0:
+                    ts(hv("m%d" % i, c), hv(raw, c), v(col, 0, 1), A.is_equal, v(neg), A.mult)
+                    tt(dst, dst, hv("m%d" % i, c), A.add)
+        tt(hv("evn", c), kv, hv("Kn", c), A.is_equal)
+        mm(v("b6", 400 + 8 * c, 408 + 8 * c), hv("evn", c), v("G8b"))
+        ts(hv("dr", c, 8), v("b6", 400 + 8 * c, 408 + 8 * c), 3.0, A.is_ge, float(DIR), A.mult)
+        tt(hv("kn", c, 8), v("b6", 384 + 8 * c, 392 + 8 * c), hv("dr", c, 8), A.add)
+        for b in range(128 * c, 128 * c + 128, 32):
+            act(v("Kc", 16 * b, 16 * b + 512), ind(old, v("BnL", b, b + 32)))
+        for q in (2 * c, 2 * c + 1):
+            for eq, b in (("eqV", 0), ("eqN", 256)):
+                for k in range(16):
+                    s = (1024 * q + k, 1024 * q + 1024, 16)
+                    tt(v(eq, *s), v("b0", b + 64 * q, b + 64 * q + 64), v("Kc", *s), A.is_equal)
+
+    def third(t, c):
+        for eq, b in (("eqV", "b2"), ("eqN", "b3")):
+            mm(v(b, 128 * c, 128 * c + 128), hv("BnC", c), v("If"), True, False)
+            for k in range(16):
+                mm(v(b, 128 * c + k, 128 * c + 128, 16), v(eq, 2048 * c + k, 2048 * c + 2048, 16), v("G8s"), False, k == 15)
+        act(hv("cV", c), v("b2", 128 * c, 128 * c + 128))
+        tt(hv("mn", c), v("b3", 128 * c, 128 * c + 128), hv("cV", c), A.min)
+        scan(hv("sc2", c), v("RN", 0, 128), hv("mn", c), A.max)
+        tt(hv("W", c, 8), v("sc2", 128 * c + 15, 128 * c + 128, 16), hv("kn", c, 8), A.max)
+        tt(hv("Aw", c), ind(hv("W", c, 8), v("bl", 0, 8)), v("DM", 0, 128), A.mult)
+        o = v("b6", 416 + 8 * c, 424 + 8 * c)
+        mm(o, hv("Aw", c), v("G8f"))
+        cp(hv("wi", c, 8), o)
+        ts(hv("wi2", c, 8), hv("wi", c, 8), SB - 1, A.bitwise_and)
+        w = vo(t + 1, c)
+        cp(w, hv("wi2", c, 8))
+        tt(hv("kp", c), ind(K(t), w), hv("V2", c), A.mult)
+        ts(hv("pl", c), hv("kp", c), 0.25, A.mult, v("pl%d" % t), A.add)
+        ts(hv("plm", c), hv("pl", c), 2047, A.bitwise_and)
+        cp(hv("PL", c), hv("plm", c))
+        for q in (2 * c, 2 * c + 1):
+            for b in (64 * q, 64 * q + 32):
+                act(v("Xc", 16 * b, 16 * b + 512), ind(v("X"), v("PL", b, b + 32)))
+            if q in PEQ:
+                for b in range(1024 * q, 1024 * q + 1024, 512):
+                    mm(v("b7"), v("Ib"), v("Xc", b, b + 512), True, False)
+                    mm(v("b7"), hv("zT", c), v("RS", b - 2048 * c, b - 2048 * c + 512), False, True)
+                    act(v("ab", b, b + 512), v("b7"), AF.Abs)
+                continue
+            for k in range(16):
+                s = (1024 * q + k, 1024 * q + 1024, 16)
+                tt(v("df", *s), v("b1", 64 * q, 64 * q + 64), v("Xc", *s), A.subtract)
+            act(v("ab", 1024 * q, 1024 * q + 1024), v("df", 1024 * q, 1024 * q + 1024), AF.Abs)
+        act(hv("Kw", c), ind(K(t), w))
+        ts(hv("hz", c), hv("Kw", c), 0.0, A.is_equal, float(2 ** 25), A.mult)
+        if t < RO - 1:
+            act(hv("Vn", c), ind(v("T1"), w))
+            act(hv("V2", c), hv("Vn", c), scale=2.0, bias=1.0)
+        tt(hv("pr", c), v("b1", 128 * c, 128 * c + 128), hv("Kw", c), A.mult)
+        mm(v("b6", 448 + 8 * c, 456 + 8 * c), hv("pr", c), v("G8f"))
+        pa = v("b5", 256 + 128 * c, 384 + 128 * c)
+        mm(pa, v("Ib"), hv("Kw", c), True, False)
+        mm(pa, v("Ib"), hv("UC", c), False, True)
+
+    def fourth(t, c):
+        dT = v("b4", 128 * c, 128 * c + 128)
+        mm(dT, v("Ib"), v("LPh"), True, False)
+        mm(dT, v("Ib"), v("LPl"), False, False)
+        for p in range(16):
+            mm(v("b4", 128 * c + p, 128 * c + 128, 16), v("ab", 2048 * c + p, 2048 * c + 2048, 16), v("G8k"), False, p == 15)
+        act(hv("dk", c), dT)
+        scan(hv("sd", c), v("RP"), dT, A.min)
+        mm(v("b5", 128 * c, 128 * c + 128), v("Ib"), hv("hz", c), True, False)
+        mm(v("b5", 128 * c, 128 * c + 128), hv("dk", c), v("If"), False, True)
+        tt(hv("Ap", c), ind(hv("sd", c), v("bl2", 0, 8)), v("DM", 0, 128), A.mult)
+        o = v("b6", 432 + 8 * c, 440 + 8 * c)
+        mm(o, hv("Ap", c), v("G8f"))
+        cp(hv("pi", c, 8), o)
+        ts(hv("pi2", c, 8), hv("pi", c, 8), 2047, A.bitwise_and)
+        do = v("dO", 16 * c, 16 * c + 8)
+        cp(do, hv("pi2", c, 8))
+        tt(hv("zx", c), ind(v("Xc", 2048 * c, 2048 * c + 2048), do), hv("z", c), A.add)
+        ts(hv("dz", c), hv("zx", c), 0.5, A.mult, -0.25, A.add)
+        zp = v("b1", 128 * c, 128 * c + 128)
+        if t == RO - 1:
+            cp(hv("zF", c), hv("dz", c))
+            store(T.yz[:, 128 * c:128 * c + 128], hv("zF", c), c)
+        else:
+            cp(hv("z", c), hv("dz", c))
+            cp(zp, hv("z", c))
+            turn(c)
+        act(hv("cd", c), v("b5", 128 * c, 128 * c + 128), AF.Relu, scale=-float(2 ** 18), bias=v("thrc"))
+        tt(hv("rr", c), v("b5", 256 + 128 * c, 384 + 128 * c), hv("cd", c), A.min)
+
+    def writers(t):
+        ts(v("F"), v("W"), float(SB), A.is_lt)
+        ts(v("Lb"), v("W"), float(DIR), A.is_lt)
+        mm(v("b2", 400, 408), v("TriO"), v("F", 0, 8))
+        mm(v("b2", 408, 416), v("TriO"), v("F", 8, 16), True, False)
+        mm(v("b2", 408, 416), v("On"), v("F", 0, 8), False, True)
+        ts(v("x96"), v("b2", 400, 416), float(CAP), A.is_ge)
+        tt(v("y96"), v("x96"), v("F"), A.mult)
+        tt(v("act"), v("Lb"), v("y96"), A.subtract)
+        wr = v("act")
+        if t:
+            for gr in range(8):
+                e, f = 256 * gr, 128 * gr
+                mm(v("b2", 416 + gr, 417 + gr), v("EA", e, e + 128), v("act", gr, gr + 1))
+                mm(v("b2", 424 + gr, 425 + gr), v("EA", e + 128, e + 256), v("act", gr, gr + 1), True, False)
+                mm(v("b2", 424 + gr, 425 + gr), v("EB", f, f + 128), v("act", 8 + gr, 9 + gr), False, True)
+            ts(v("wr"), v("b2", 416, 432), 0.0, A.is_equal)
+            tt(v("wr2"), v("wr"), v("act"), A.mult)
+            wr = v("wr2")
+        cp(v("Wi"), v("W"))
+        ts(v("wT"), v("Wi"), SB - 1, A.bitwise_and)
+        cp(v("hi"), v("b6", 448, 464))
+        ts(v("h2"), v("hi"), 1023, A.bitwise_and)
+        tt(v("ha"), v("h2"), v("wT"), A.subtract)
+        ts(v("hb"), v("ha"), float(REM + 1024 * t), A.add)
+        tt(v("hc"), v("hb"), v("F"), A.mult)
+        tt(v("src"), v("hc"), v("wT"), A.add)
+        tt(v("w2"), wr, v("vmd4"), A.mult)
+        tt(v("hb"), v("w2"), v("d04"), A.add)
+        tt(v("word"), v("hb"), v("src"), A.add)
+        tt(v("Aq"), ind(v("word"), v("bl")), v("DM"), A.mult)
+        for c in range(2):
+            mm(v("b2", 448 + 8 * c, 456 + 8 * c), hv("Aq", c), v("G8f"))
+        cp(v("qi"), v("b2", 448, 464))
+        ts(v("q1"), v("qi"), 13, A.arith_shift_right)
+        cp(v("scO"), v("q1"))
+        ts(v("q2"), v("qi"), 8191, A.bitwise_and)
+        cp(v("srO"), v("q2"))
+        act(v("hole"), v("b0", 0, 256), AF.Relu, scale=-1.0)
+        act(v("Kvr"), v("b0", 0, 256), AF.Relu)
+        kk = "KK%d" % (t % 2)
+        tt(v("fm"), ind(v(kk, 0, REM + 1024 * (t + 1)), v("srO")), v("hole"), A.mult)
+        tt(ind(v(kk, 0, REM), v("scO")), v("fm"), v("Kvr"), A.add)
+        if t < RO - 1:
+            tt(v("ohw"), v("b1", 256, 512), v("Vn"), A.mult)
+            tt(ind(v("B"), v("scO")), v("Bk"), v("ohw"), A.add)
+            mm(v("b2", 432, 448), v("On"), v("F"))
+            act(v("fj"), v("b2", 432, 448), accum_out=v("fs"))
+            cp(v("fi"), v("fs"))
+            ts(v("fa"), v("fi"), 15, A.bitwise_and)
+            ts(v("t1"), v("wT"), 8192.0, A.mult)
+            tt(v("vmd4"), v("t1"), v("d04"), A.subtract)
+
+    def same_node():
+        ts(v("ci"), v("Vn"), v("p2"), A.mult, v("dcol"), A.add)
+        ts(v("cb"), v("ci"), 1, A.bitwise_and)
+        ts(v("code"), v("cb"), -2.0, A.mult, 1.0, A.add)
+        act(v("cdE"), v("code"), scale=v("even"))
+        act(v("cdO"), v("code"), scale=v("odd"))
+        for gr in range(8):
+            lo = 32 * (gr // 2)
+            m = "cdO" if gr % 2 else "cdE"
+            b = "b3" if gr % 2 else "b7"
+            mm(v(b, 0, 256), v(m, 0, 128, 1, lo, lo + 32), v("code", 0, 256, 1, lo, lo + 32))
+            mm(v(b, 256, 384), v(m, 128, 256, 1, lo, lo + 32), v("code", 128, 256, 1, lo, lo + 32))
+            act(v("E0", 256 * gr, 256 * gr + 256), v(b, 0, 256), AF.Relu, bias=v("fb"))
+            act(v("E1", 128 * gr, 128 * gr + 128), v(b, 256, 384), AF.Relu, bias=v("fb"))
+        for e, o, w in (("E0", "EA", 256), ("E1", "EB", 128)):
+            op("g", "affine_select", out=v(o), in_=v(e), pattern=[[0, 8], [1, w]], compare_op=A.is_gt, fill=0.0, base=0,
+               channel_multiplier=-1)
+
+    def revoke(t):
+        if t:
+            come = v("cI%d" % (t - 1), 0, 1)
+            ts(v("ncome"), come, -1.0, A.mult)
+            if t < RO - 1:
+                ts(v("gb"), come, 0.0, A.is_gt)
+                tt(v("gc"), v("ncome"), v("gb"), A.subtract)
+            ts(v("NM2"), K(t), come, A.is_equal, v("ncome"), A.mult)
+        op("v", "tensor_reduce", out=v("rvm"), in_=v("rr"), axis=AxisListType.X, op=A.max)
+        cp(v("rvi"), v("rvm"))
+        ts(v("rva"), v("rvi"), 255, A.bitwise_and)
+        rv = v("rS%d" % t, 0, 1)
+        cp(rv, v("rva"))
+        if t:
+            ts(v("rvE%d" % t), rv, v("cI%d" % (t - 1), 0, 1), A.not_equal, rv, A.mult)
+        else:
+            cp(v("rvE0"), v("rva"))
+        rv = v("rvE%d" % t)
+        ts(v("nrv"), rv, -1.0, A.mult)
+        if t < RO - 1:
+            ts(v("ga"), rv, 0.0, A.is_gt)
+            tt(v("gr"), v("nrv"), v("ga"), A.subtract)
+        kk = "KK%d" % (t % 2)
+        blocks = ((0, 512, "b4"), (512, 1024, "b7"), (1024, 1280, "b4"))
+        for lo, hi, b in blocks:
+            ts(v("NM1", lo, hi), v(kk, lo, hi), rv, A.is_equal, v("nrv"), A.mult)
+        for lo, hi, b in blocks:
+            o = v(b, 0, hi - lo)
+            mm(o, v("Ib"), v(kk, lo, hi), True, False)
+            if t:
+                mm(o, v("Ib"), v("NM2", lo, hi), False, False)
+            mm(o, v("Ib"), v("NM1", lo, hi), False, True)
+            if t == RO - 1:
+                act(v("Yk", lo, hi), o)
+                store(T.yk[:, lo:hi], v("Yk", lo, hi), 2 + lo // 512)
+            else:
+                act(v("KK%d" % ((t + 1) % 2), lo, hi), o)
+        if t < RO - 1:
+            send_revoked(t)
+            send_rings(t + 1)
+            ts(v("thrc"), v("fa"), v("thr"), A.add, float(2 ** 30), A.mult)
+
+    send_rings(0)
+    for c in range(2):
+        first(0, c)
+    for t in range(RO):
+        for c in range(2):
+            second(t, c)
+        for c in range(2):
+            third(t, c)
+        writers(t)
+        fourth(t, 0)
+        if t < RO - 1:
+            first(t + 1, 0)
+        fourth(t, 1)
+        revoke(t)
+        if t < RO - 1:
+            first(t + 1, 1)
+            same_node()
+    if not SEQ:
+        SEQ.append(order(ops))
+    issue(g, T, ops, SEQ[0])
+
+
+def hand_on(g, core, T, topo):
+    n = len(T.cores)
+    for r in range(n):
+        src, below, above = T.cores[r], T.cores[(r - 1) % n], T.cores[(r + 1) % n]
+        rl = relays(src, T, topo, below)
+        rv_relay = relays(src, T, topo, above)[0]
+        if core not in rl and core != rv_relay:
+            continue
+        for t in range(RO):
+            if t and core == rv_relay:
+                g.wait_ge(T.sem["ra%d" % (t - 1)], 8)
+                remote(g, topo, core, above, T["cI%d" % (t - 1)][:, 0:1], T["hrv%d" % (t - 1)][:, 0:1],
+                       T.sem["ri%d" % (t - 1)], T.sem["rl%d" % (t - 1)], 8)
+            if core in rl:
+                h = rl.index(core)
+                g.wait_ge(T.sem["ha%d" % t], 8)
+                lo = REM + 1024 * t + 512 * h
+                remote(g, topo, core, below, T["KK%d" % (t % 2)][:, lo:lo + 512], T["hand%d" % t][:],
+                       T.sem["ki%d%d" % (t, h)], T.sem["hs%d" % t], 8)
+        for t in range(RO):
+            if core in rl:
+                g.wait_ge(T.sem["hs%d" % t], 8)
+            if t and core == rv_relay:
+                g.wait_ge(T.sem["rl%d" % (t - 1)], 8)

@@ -14,13 +14,13 @@ DIR = 239 * SB
 F32 = dict(If=128, G16f=128, G8f=8, DM=256, RN=256, RP=128, T1=1280, B=1536, Bv=256, mB=256, Bk=256, dg=256, sc=256, BnC=256,
            dr=16, kn=16, cV=256, mn=256, sc2=256, W=16, Aw=256, kp=256, Vn=256, V2=256, pr=256, zx=256, sd=256,
            Ap=256, dk=256, cd=256, rr=256, ohw=256, zF=256, pcol=1, p2=1, p2b=1, dcol=1, odd=1, even=1, kcol=1, thr=1, thrc=1,
-           nrv=1, rvE0=1, rvE1=1, rvE2=1, ga=1, gb=1, gr=1, gc=1, rvm=1, ncome=1, fs=1, fj=16, d04=16, vmd4=16, x96=16, y96=16,
-           wr=16, wr2=16, ha=16, hb=16, hc=16, src=16, w2=16, word=16, t1=16, Aq=256, pm0=1, pm1=1, pm2=1, pl0=1, pl1=1, pl2=1,
+           nrv=1, rvE1=1, rvE2=1, ncome=1, fs=1, fj=16, d04=16, vmd4=16, x96=16, av=16, hd=16,
+           wr=16, hb=16, hc=16, src=16, w2=16, word=16, t1=16, Aq=256, pm0=1, pm1=1, pm2=1, pl0=1, pl1=1, pl2=1,
            p5=1, fb=1)
 BF = dict(Ib=128, G16b=128, G8b=8, G8s=8, G8k=8, TriO=128, On=128, LPh=128, LPl=128, UC=256, z=256, Kv=256, Kn=256,
-          Kw=256, evn=256, m0=256, m1=256, Kvr=256, zT=256, hz=256, hole=256, fm=256, code=256, cdE=256, cdO=256, F=16, Lb=16,
+          Kw=256, evn=256, m0=256, m1=256, Kvr=256, zT=256, hz=256, sgn=256, hole=256, fm=256, code=256, cdE=256, cdO=256, F=16, NF=16, Lb=16,
           act=16, NM1=1280, NM2=1280)
-I32 = dict(PI=1, pi15=1, pb=1, D1=256, D15=256, D2=128, D3=256, ic=16, iv=16, y1=256, y2=256, wi=16, wi2=16, pl=256, plm=256,
+I32 = dict(PI=1, pi15=1, pb=1, D1=256, D15=256, D2=128, D3=256, ic=16, iv=16, y1=256, y2=256, pl=256, plm=256,
            pi=16, pi2=16, dz=256, Wi=16, wT=16, hi=16, h2=16, qi=16, q1=16, q2=16, rvi=1, rva=1, fi=1, fa=1, ci=256, cb=256)
 U16 = dict(bl=16, bl2=16, vO=32, nO=32, wO=32, scO=16, srO=16, dO=32, BnL=256, PL=256)
 
@@ -67,6 +67,12 @@ for _t in range(RO - 1):
 
 CY = 0.00083
 SEQ = []
+TAIL = 0.16
+SIG, SEED, WIN = 0.02, 1080, 0.0
+
+
+def noise(i, seed):
+    return ((i * 2654435761 + seed * 1013904223 + (i ^ seed) * 69069) % 65521) / 65521.0 - 0.5
 
 
 def relays(core, T, topo, dst):
@@ -232,7 +238,7 @@ def noter(T):
             if m == "affine_select":
                 return e.affine_select(**a)
             return e.iota(**a)
-        i = rec(q, cost(q, m, kw), 0.06, reads, writes, emit)
+        i = rec(q, cost(q, m, kw), TAIL, reads, writes, emit)
         if m == "matmul":
             b = kw["out"][1]
             if b in opened:
@@ -265,6 +271,7 @@ def order(ops):
         for u, w in users[i]:
             b = max(b, prio[u] + (ops[i][2] if w else 0.0))
         prio[i] = b + ops[i][1]
+    prio = [p * (1 + SIG * noise(i, SEED)) for i, p in enumerate(prio)]
     ready = [0.0] * n
     avail = {}
     free = {}
@@ -279,7 +286,7 @@ def order(ops):
                 continue
             f = free.get(q, 0.0)
             s0 = min(max(f, ready[i]) for i in avail[q])
-            i = max((i for i in avail[q] if max(f, ready[i]) <= s0 + 0.03), key=lambda k: (prio[k], -k))
+            i = max((i for i in avail[q] if max(f, ready[i]) <= s0 + WIN), key=lambda k: (prio[k], -k))
             s = max(f, ready[i])
             if best is None or s < best[0]:
                 best = (s, q, i)
@@ -488,23 +495,26 @@ def rank_program(g, core, T, topo):
         return v("vO", b + 8 * c, b + 8 * c + 8)
 
     def first(t, c):
-        act(hv("Bv", c), ind(v("B", 0, 1280), vo(t, c)))
+        tab = v("B", 0, 1280) if t else v("NBi")
+        bv = hv("Bv", c) if t else v("NBi", 640 * c, 640 * c + 640, 5)
+        if t:
+            act(bv, ind(tab, vo(t, c)))
         mm(v("b6", 0, 128), v("G16b"), hv("z", c))
         ts(hv("y1", c), v("b6", 0, 128), v("pm%d" % t), A.add)
         ts(hv("y2", c), hv("y1", c), 15, A.bitwise_and)
         oh = v("b1", 256 + 128 * c, 384 + 128 * c)
         ts(oh, hv("y2", c), 0.0, A.is_equal)
-        tt(hv("mB", c), oh, hv("Bv", c), A.mult)
+        tt(hv("mB", c), oh, bv, A.mult)
         nr = v("b6", 128 + 128 * c, 256 + 128 * c)
         mm(nr, v("G16f"), hv("mB", c))
         mm(v("b6", 384 + 8 * c, 392 + 8 * c), hv("mB", c), v("G8f"))
         tt(hv("dg", c), nr, hv("DM", c), A.mult)
         scan(hv("sc", c), hv("RN", c), hv("dg", c), A.max)
         cp(v("nO", 16 * c, 16 * c + 8), v("sc", 128 * c + 15, 128 * c + 128, 16))
-        cp(hv("BnL", c), ind(v("B", 0, 1280), v("nO", 16 * c, 16 * c + 8)))
+        cp(hv("BnL", c), ind(tab, v("nO", 16 * c, 16 * c + 8)))
         ts(hv("BnC", c), hv("BnL", c), v("kcol"), A.add)
         if t < RO - 1:
-            tt(hv("Bk", c), hv("Bv", c), hv("mB", c), A.subtract)
+            tt(hv("Bk", c), bv, hv("mB", c), A.subtract)
 
     def second(t, c):
         kv, kn = v("b0", 128 * c, 128 * c + 128), v("b0", 256 + 128 * c, 384 + 128 * c)
@@ -517,9 +527,9 @@ def rank_program(g, core, T, topo):
                 tt(dst, dst, hv(raw, c), A.add)
             else:
                 ts(dst, hv(raw, c), 0.25, A.max)
-            for i, col, neg in ((0, "cI%d" % (t - 2), "gc"), (1, "rvE%d" % (t - 1), "gr")):
+            for i, col in ((0, "cI%d" % (t - 2)), (1, "rS%d" % (t - 1))):
                 if t - 2 + i >= 0:
-                    ts(hv("m%d" % i, c), hv(raw, c), v(col, 0, 1), A.is_equal, v(neg), A.mult)
+                    ts(hv("m%d" % i, c), hv(raw, c), v(col, 0, 1), A.is_equal, -1024.0, A.mult)
                     tt(dst, dst, hv("m%d" % i, c), A.add)
         tt(hv("evn", c), kv, hv("Kn", c), A.is_equal)
         mm(v("b6", 400 + 8 * c, 408 + 8 * c), hv("evn", c), v("G8b"))
@@ -542,13 +552,13 @@ def rank_program(g, core, T, topo):
         tt(hv("mn", c), v("b3", 128 * c, 128 * c + 128), hv("cV", c), A.min)
         scan(hv("sc2", c), v("RN", 0, 128), hv("mn", c), A.max)
         tt(hv("W", c, 8), v("sc2", 128 * c + 15, 128 * c + 128, 16), hv("kn", c, 8), A.max)
-        tt(hv("Aw", c), ind(hv("W", c, 8), v("bl", 0, 8)), v("DM", 0, 128), A.mult)
+        cp(hv("Wi", c, 8), hv("W", c, 8))
+        ts(hv("wT", c, 8), hv("Wi", c, 8), SB - 1, A.bitwise_and)
+        tt(hv("Aw", c), ind(hv("wT", c, 8), v("bl", 0, 8)), v("DM", 0, 128), A.mult)
         o = v("b6", 416 + 8 * c, 424 + 8 * c)
         mm(o, hv("Aw", c), v("G8f"))
-        cp(hv("wi", c, 8), o)
-        ts(hv("wi2", c, 8), hv("wi", c, 8), SB - 1, A.bitwise_and)
         w = vo(t + 1, c)
-        cp(w, hv("wi2", c, 8))
+        cp(w, o)
         tt(hv("kp", c), ind(K(t), w), hv("V2", c), A.mult)
         ts(hv("pl", c), hv("kp", c), 0.25, A.mult, v("pl%d" % t), A.add)
         ts(hv("plm", c), hv("pl", c), 2047, A.bitwise_and)
@@ -609,14 +619,23 @@ def rank_program(g, core, T, topo):
 
     def writers(t):
         ts(v("F"), v("W"), float(SB), A.is_lt)
+        ts(v("NF"), v("W"), float(SB), A.is_ge, -512.0, A.mult)
         ts(v("Lb"), v("W"), float(DIR), A.is_lt)
-        mm(v("b2", 400, 408), v("TriO"), v("F", 0, 8))
+        mm(v("b2", 400, 408), v("TriO"), v("F", 0, 8), True, False)
+        mm(v("b2", 400, 408), v("Ib"), v("NF", 0, 8), False, True)
         mm(v("b2", 408, 416), v("TriO"), v("F", 8, 16), True, False)
+        mm(v("b2", 408, 416), v("Ib"), v("NF", 8, 16), False, False)
         mm(v("b2", 408, 416), v("On"), v("F", 0, 8), False, True)
-        ts(v("x96"), v("b2", 400, 416), float(CAP), A.is_ge)
-        tt(v("y96"), v("x96"), v("F"), A.mult)
-        tt(v("act"), v("Lb"), v("y96"), A.subtract)
-        wr = v("act")
+        ts(v("x96"), v("b2", 400, 416), float(CAP), A.is_lt)
+        tt(v("act"), v("x96"), v("Lb"), A.mult)
+        tt(v("av"), v("act"), v("vmd4"), A.mult)
+        cp(v("hi"), v("b6", 448, 464))
+        ts(v("h2"), v("hi"), 1023, A.bitwise_and)
+        ts(v("hb"), v("h2"), float(REM + 1024 * t), A.add)
+        tt(v("hc"), v("hb"), v("F"), A.mult)
+        tt(v("src"), v("hc"), v("wT"), A.max)
+        tt(v("hd"), v("src"), v("d04"), A.add)
+        w2 = v("av")
         if t:
             for gr in range(8):
                 e, f = 256 * gr, 128 * gr
@@ -624,19 +643,9 @@ def rank_program(g, core, T, topo):
                 mm(v("b2", 424 + gr, 425 + gr), v("EA", e + 128, e + 256), v("act", gr, gr + 1), True, False)
                 mm(v("b2", 424 + gr, 425 + gr), v("EB", f, f + 128), v("act", 8 + gr, 9 + gr), False, True)
             ts(v("wr"), v("b2", 416, 432), 0.0, A.is_equal)
-            tt(v("wr2"), v("wr"), v("act"), A.mult)
-            wr = v("wr2")
-        cp(v("Wi"), v("W"))
-        ts(v("wT"), v("Wi"), SB - 1, A.bitwise_and)
-        cp(v("hi"), v("b6", 448, 464))
-        ts(v("h2"), v("hi"), 1023, A.bitwise_and)
-        tt(v("ha"), v("h2"), v("wT"), A.subtract)
-        ts(v("hb"), v("ha"), float(REM + 1024 * t), A.add)
-        tt(v("hc"), v("hb"), v("F"), A.mult)
-        tt(v("src"), v("hc"), v("wT"), A.add)
-        tt(v("w2"), wr, v("vmd4"), A.mult)
-        tt(v("hb"), v("w2"), v("d04"), A.add)
-        tt(v("word"), v("hb"), v("src"), A.add)
+            tt(v("w2"), v("wr"), v("av"), A.mult)
+            w2 = v("w2")
+        tt(v("word"), w2, v("hd"), A.add)
         tt(v("Aq"), ind(v("word"), v("bl")), v("DM"), A.mult)
         for c in range(2):
             mm(v("b2", 448 + 8 * c, 456 + 8 * c), hv("Aq", c), v("G8f"))
@@ -645,7 +654,8 @@ def rank_program(g, core, T, topo):
         cp(v("scO"), v("q1"))
         ts(v("q2"), v("qi"), 8191, A.bitwise_and)
         cp(v("srO"), v("q2"))
-        act(v("hole"), v("b0", 0, 256), AF.Relu, scale=-1.0)
+        act(v("sgn"), v("b0", 0, 256), AF.Sign)
+        act(v("hole"), v("sgn"), AF.Relu, scale=-1.0)
         act(v("Kvr"), v("b0", 0, 256), AF.Relu)
         kk = "KK%d" % (t % 2)
         tt(v("fm"), ind(v(kk, 0, REM + 1024 * (t + 1)), v("srO")), v("hole"), A.mult)
@@ -682,24 +692,15 @@ def rank_program(g, core, T, topo):
         if t:
             come = v("cI%d" % (t - 1), 0, 1)
             ts(v("ncome"), come, -1.0, A.mult)
-            if t < RO - 1:
-                ts(v("gb"), come, 0.0, A.is_gt)
-                tt(v("gc"), v("ncome"), v("gb"), A.subtract)
             ts(v("NM2"), K(t), come, A.is_equal, v("ncome"), A.mult)
-        op("v", "tensor_reduce", out=v("rvm"), in_=v("rr"), axis=AxisListType.X, op=A.max)
-        cp(v("rvi"), v("rvm"))
+        op("v", "tensor_reduce", out=v("rvi"), in_=v("rr"), axis=AxisListType.X, op=A.max)
         ts(v("rva"), v("rvi"), 255, A.bitwise_and)
         rv = v("rS%d" % t, 0, 1)
         cp(rv, v("rva"))
         if t:
             ts(v("rvE%d" % t), rv, v("cI%d" % (t - 1), 0, 1), A.not_equal, rv, A.mult)
-        else:
-            cp(v("rvE0"), v("rva"))
-        rv = v("rvE%d" % t)
+            rv = v("rvE%d" % t)
         ts(v("nrv"), rv, -1.0, A.mult)
-        if t < RO - 1:
-            ts(v("ga"), rv, 0.0, A.is_gt)
-            tt(v("gr"), v("nrv"), v("ga"), A.subtract)
         kk = "KK%d" % (t % 2)
         blocks = ((0, 512, "b4"), (512, 1024, "b7"), (1024, 1280, "b4"))
         for lo, hi, b in blocks:

from concourse.bass import DstId, RemoteDMATransfer
from concourse.mybir import dt, AluOpType, AxisListType, ActivationFunctionType
import comms_topo

A = AluOpType
AF = ActivationFunctionType
RO, SB, CAP = 3, 2048, 96
BIG = 1.0e9
PEQ = (0, 2)
REM = 1536
WS = 17 * SB
DIR = 239 * SB

F32 = dict(If=128, G16f=128, G8f=8, DM=256, RN=256, RP=128, T1=1280, B=1536, Bv=256, mB=256, Bk=256, dg=256, sc=256, BnC=256,
           dr=16, kn=16, cV=256, mn=256, sc2=256, W=16, Aw=256, kp=256, Vn=256, V2=256, pr=256, zx=256, sd=256,
           Ap=256, dk=256, cd=256, rr=256, ohw=256, zF=256, pcol=1, p2=1, p2b=1, dcol=1, odd=1, even=1, kcol=1, thr=1, thrc=1,
           nrv=1, rvE1=1, rvE2=1, ncome=1, fs=1, fj=16, d04=16, vmd4=16, x96=16, av=16, hd=16,
           wr=16, hb=16, hc=16, src=16, w2=16, word=16, t1=16, Aq=256, pm0=1, pm1=1, pm2=1, pl0=1, pl1=1, pl2=1,
           p5=1, fb=1)
BF = dict(Ib=128, G16b=128, G8b=8, G8s=8, G8k=8, TriO=128, On=128, LPh=128, LPl=128, UC=256, z=256, Kv=256, Kn=256,
          Kw=256, evn=256, m0=256, m1=256, Kvr=256, zT=256, hz=256, sgn=256, hole=256, fm=256, code=256, cdE=256, cdO=256, F=16, NF=16, Lb=16,
          act=16, NM1=1280, NM2=1280)
I32 = dict(PI=1, pi15=1, pb=1, D1=256, D15=256, D2=128, D3=256, ic=16, iv=16, y1=256, y2=256, pl=256, plm=256,
           pi=16, pi2=16, dz=256, Wi=16, wT=16, hi=16, h2=16, qi=16, q1=16, q2=16, rvi=1, rva=1, fi=1, fa=1, ci=256, cb=256)
U16 = dict(bl=16, bl2=16, vO=32, nO=32, wO=32, scO=16, srO=16, dO=32, BnL=256, PL=256)


def _layout(d):
    pos, at = {}, 0
    for n in d:
        pos[n] = at
        at += (d[n] + 15) // 16 * 16
    return pos, at


_PF, _NF = _layout(F32)
_PB, _NB = _layout(BF)
_PI, _NI = _layout(I32)
_PU, _NU = _layout(U16)
WHERE = {}
for _d, _p, _n in ((F32, _PF, "SF"), (BF, _PB, "SBF"), (I32, _PI, "SI"), (U16, _PU, "SU")):
    for _k in _d:
        WHERE[_k] = (_n, _p[_k], _d[_k])
_BIGB = dict(KK0=(REM + 1024 * RO, "bfloat16"), KK1=(REM + 1024 * RO, "bfloat16"), RS=(2048, "bfloat16"), X=(2048, "bfloat16"),
             Kc=(4096, "bfloat16"), eqV=(4096, "bfloat16"), eqN=(4096, "bfloat16"), Xc=(4096, "bfloat16"), df=(4096, "bfloat16"),
             ab=(4096, "bfloat16"), EA=(2048, "bfloat16"), EB=(1024, "bfloat16"), E0=(2048, "bfloat16"), E1=(1024, "bfloat16"),
             NBi=(1280, "int32"), Yk=(1280, "bfloat16"), thI=(8, "int32"), rS0=(8, "float32"), rS1=(8, "float32"),
             rS2=(8, "float32"), cI0=(8, "float32"), cI1=(8, "float32"))
SCRATCH = {"SF": ("sbuf", [128, _NF], "float32"), "SBF": ("sbuf", [128, _NB], "bfloat16"), "SI": ("sbuf", [128, _NI], "int32"),
           "SU": ("sbuf", [128, _NU], "uint16")}
for _k in _BIGB:
    SCRATCH[_k] = ("sbuf", [128, _BIGB[_k][0]], _BIGB[_k][1])
    WHERE[_k] = (_k, 0, _BIGB[_k][0])
for _k in range(8):
    SCRATCH["b%d" % _k] = ("psum", [128, 512], "float32")
    WHERE["b%d" % _k] = ("b%d" % _k, 0, 512)
for _k in range(RO):
    SCRATCH["hand%d" % _k] = ("sbuf", [128, 512], "bfloat16")
for _k in range(RO - 1):
    SCRATCH["hrv%d" % _k] = ("sbuf", [128, 8], "float32")
SEMAPHORES = ["qv", "qs", "qt", "qg"]
SEMAPHORES += ["ld%d" % i for i in range(8)] + ["st%d" % i for i in range(5)]
for _t in range(RO):
    SEMAPHORES += ["ks%d0" % _t, "ks%d1" % _t, "ki%d0" % _t, "ki%d1" % _t, "ha%d" % _t, "hs%d" % _t]
for _t in range(RO - 1):
    SEMAPHORES += ["rs%d" % _t, "ri%d" % _t, "ra%d" % _t, "rl%d" % _t]

CY = 0.00083
SEQ = []
TAIL = 0.16
SIG, SEED, WIN = 0.02, 1080, 0.0


def noise(i, seed):
    return ((i * 2654435761 + seed * 1013904223 + (i ^ seed) * 69069) % 65521) / 65521.0 - 0.5


def relays(core, T, topo, dst):
    out = []
    for d in (topo.die(core), 1 - topo.die(core)):
        for c in topo.cores_of(core):
            if c != core and topo.die(c) == d and T.rank_of(c) is None and topo.may_write(c, dst):
                out.append(c)
                break
    return out


def engines_mask(topo, src, dst, n):
    m = 0
    for e in topo.engines(src, dst)[:n]:
        m |= 1 << e
    return m


def remote(g, topo, src, dst, out, in_, rsem, lsem, n):
    rid, pid = topo.addr(dst, src)
    return g.remote_dma(out, in_, rsem, lsem, pid, rid, engines_mask(topo, src, dst, n))


def view(name, lo=0, hi=None, step=1, plo=0, phi=128):
    return ("@", name, lo, WHERE[name][2] if hi is None else hi, step, plo, phi)


def ind(win, off):
    return ("#", win, off)


def is_view(x):
    return isinstance(x, tuple) and len(x) > 0 and (x[0] == "@" or x[0] == "#")


def count(x):
    if x[0] == "#":
        return 16 * (x[2][3] - x[2][2])
    return (x[3] - x[2] + x[4] - 1) // x[4]


def psum(x):
    return x[0] == "@" and x[1][0] == "b" and len(x[1]) == 2 and x[1][1].isdigit()


def two(x):
    return x[0] == "@" and WHERE[x[1]][0] not in ("SF", "SI", "NBi", "thI") and not psum(x)


def clash(a, b):
    if a[3] <= b[2] or b[3] <= a[2] or a[6] <= b[5] or b[6] <= a[5]:
        return False
    if a[4] > 1 and a[4] == b[4] and (a[2] - b[2]) % a[4]:
        return False
    return True


def covers(a, b):
    return a[4] == 1 and a[2] <= b[2] and a[3] >= b[3] and a[5] <= b[5] and a[6] >= b[6]


def cost(q, m, kw):
    o = kw.get("out")
    if q == "t":
        n, mm = count(kw["rhs"]), count(kw["lhsT"])
        f = 4 if WHERE[kw["lhsT"][1]][0] == "SF" else 1
        return max(min(64, mm), n) * f * CY
    if q == "g":
        return 0.15 + 2 * count(o) * CY
    ins = [kw[k] for k in kw if k not in ("out", "accum_out") and is_view(kw[k])]
    full = [i for i in ins if count(i) > 1]
    n = max([count(o)] + [count(i) for i in full])
    if o[0] == "#":
        return 0.05 + n * 3.8 * CY
    for i in full:
        if i[0] == "#":
            return 0.06 + n * 1.56 * CY
    c = 1.0
    if q == "v" and m == "tensor_tensor" and not psum(o) and not [i for i in full if psum(i)]:
        c = 2.0
    if q == "v" and m in ("tensor_copy", "tensor_scalar", "memset") and two(o) and not [i for i in full if not two(i)]:
        c = 0.5
    return max(64, n * c) * CY


def noter(T):
    ops, hist, opened = [], {}, {}

    def res(x):
        if x[0] == "#":
            return res(x[1]).indirect(res(x[2]))
        b, off, _ = WHERE[x[1]]
        lo, hi = off + x[2], off + x[3]
        if x[4] > 1:
            return T[b][x[5]:x[6], lo:range(lo, hi, x[4])[-1] + 1:x[4]]
        return T[b][x[5]:x[6], lo:hi]

    def touch(i, q, v, wr, deps):
        ps = psum(v)
        keep = []
        for e in hist.setdefault(v[1], []):
            ev, ew, eq, ei = e
            if ei == i:
                keep.append(e)
                continue
            if ps and eq != q:
                deps.add((ei, True))
                if wr and covers(v, ev):
                    continue
            elif (wr or ew) and clash(v, ev):
                if not (ps and q == "t"):
                    deps.add((ei, True))
                if wr and covers(v, ev):
                    continue
            keep.append(e)
        keep.append((v, wr, q, i))
        hist[v[1]] = keep

    def rec(q, c, tail, reads, writes, emit, sem=None, inc=1):
        i = len(ops)
        deps = set()
        for v in reads:
            touch(i, q, v, False, deps)
        for v in writes:
            touch(i, q, v, True, deps)
        ops.append([q, c, tail, deps, emit, sem or "q" + q, inc])
        return i

    def op(q, m, **kw):
        reads, writes = [], []
        for k in kw:
            x = kw[k]
            if not is_view(x):
                continue
            w = k in ("out", "accum_out")
            if x[0] == "#":
                (writes if w else reads).append(x[1])
                reads.append(x[2])
            else:
                (writes if w else reads).append(x)

        def emit(e):
            a = {}
            for k in kw:
                a[k] = res(kw[k]) if is_view(kw[k]) else kw[k]
            if m == "memset":
                return e.memset(a["out"], a["constant"])
            if m == "tensor_copy":
                return e.tensor_copy(a["out"], a["in_"])
            if m == "tensor_tensor":
                return e.tensor_tensor(**a)
            if m == "tensor_scalar":
                return e.tensor_scalar(**a)
            if m == "tensor_reduce":
                return e.tensor_reduce(**a)
            if m == "tensor_tensor_scan":
                return e.tensor_tensor_scan(**a)
            if m == "matmul":
                return e.matmul(**a)
            if m == "activation":
                return e.activation(**a)
            if m == "affine_select":
                return e.affine_select(**a)
            return e.iota(**a)
        i = rec(q, cost(q, m, kw), TAIL, reads, writes, emit)
        if m == "matmul":
            b = kw["out"][1]
            if b in opened:
                for j in (opened[b] if kw["start"] or kw["stop"] else opened[b][:1]):
                    ops[i][3].add((j, False))
            if kw["start"] or kw["stop"]:
                opened[b] = [i]
            else:
                opened[b].append(i)
        return i

    def land(v, sem, inc, i):
        j = rec("x", 0.0, 8.0, [], [v], None, sem, inc)
        ops[j][3].add((i, True))

    return ops, op, rec, land, res


def order(ops):
    n = len(ops)
    users = [[] for _ in range(n)]
    left = [0] * n
    for i in range(n):
        for j, w in ops[i][3]:
            users[j].append((i, w))
            left[i] += 1
    prio = [0.0] * n
    for i in range(n - 1, -1, -1):
        b = 0.0
        for u, w in users[i]:
            b = max(b, prio[u] + (ops[i][2] if w else 0.0))
        prio[i] = b + ops[i][1]
    prio = [p * (1 + SIG * noise(i, SEED)) for i, p in enumerate(prio)]
    ready = [0.0] * n
    avail = {}
    free = {}
    for i in range(n):
        if left[i] == 0:
            avail.setdefault(ops[i][0], []).append(i)
    out = []
    while len(out) < n:
        best = None
        for q in avail:
            if not avail[q]:
                continue
            f = free.get(q, 0.0)
            s0 = min(max(f, ready[i]) for i in avail[q])
            i = max((i for i in avail[q] if max(f, ready[i]) <= s0 + WIN), key=lambda k: (prio[k], -k))
            s = max(f, ready[i])
            if best is None or s < best[0]:
                best = (s, q, i)
        s, q, i = best
        avail[q].remove(i)
        free[q] = s + ops[i][1] if q != "x" else 0.0
        out.append(i)
        for u, w in users[i]:
            ready[u] = max(ready[u], s + (ops[i][1] + ops[i][2] if w else 0.0))
            left[u] -= 1
            if left[u] == 0:
                avail.setdefault(ops[u][0], []).append(u)
    return out


def issue(g, T, ops, seq):
    Q = {"v": g.vector, "s": g.scalar, "t": g.tensor, "g": g, "y": g.sync, "S": g.scalar}
    total, tok, know = {}, {}, {}
    for q in Q:
        know[q] = {}
    know["S"] = know["s"]
    for i in seq:
        q, c, tail, deps, emit, sem, inc = ops[i]
        if emit is None:
            total[sem] = total.get(sem, 0) + inc
            tok[i] = (sem, total[sem], {})
            continue
        k = know[q]
        need = {}
        for j, w in deps:
            if w:
                s, v, sn = tok[j]
                if k.get(s, 0) < v and (s not in need or need[s][0] < v):
                    need[s] = (v, sn)
        for s in sorted(need):
            v, sn = need[s]
            if [o for o in need if o != s and need[o][1].get(s, 0) >= v]:
                continue
            Q[q].wait_ge(T.sem[s], v)
        for s in need:
            v, sn = need[s]
            k[s] = max(k.get(s, 0), v)
            for o in sn:
                k[o] = max(k.get(o, 0), sn[o])
        total[sem] = total.get(sem, 0) + inc
        r = emit(Q[q])
        if r is not None:
            r.then_inc(T.sem[sem], inc)
        tok[i] = (sem, total[sem], dict(k))
    for s in sorted(total):
        if know["g"].get(s, 0) < total[s]:
            g.wait_ge(T.sem[s], total[s])


def rank_program(g, core, T, topo):
    rank = T.rank_of(core)
    n = len(T.cores)
    if rank is None:
        hand_on(g, core, T, topo)
        return
    ops, op, rec, land, res = noter(T)
    below, above = T.cores[(rank - 1) % n], T.cores[(rank + 1) % n]
    rl = relays(core, T, topo, below)
    rv_relay = relays(core, T, topo, above)[0]
    v = view

    def tt(out, a, b, o):
        return op("v", "tensor_tensor", out=out, in0=a, in1=b, op=o)

    def ts(out, a, s1, o1, s2=None, o2=None):
        if o2 is None:
            return op("v", "tensor_scalar", out=out, in0=a, scalar1=s1, scalar2=None, op0=o1)
        return op("v", "tensor_scalar", out=out, in0=a, scalar1=s1, scalar2=s2, op0=o1, op1=o2)

    def cp(out, a):
        return op("v", "tensor_copy", out=out, in_=a)

    def act(out, a, f=AF.Copy, **kw):
        return op("s", "activation", out=out, in_=a, func=f, **kw)

    def mm(out, l, r, start=True, stop=True):
        return op("t", "matmul", out=out, lhsT=l, rhs=r, start=start, stop=stop)

    def iota(out, pattern, base, cm):
        kw = dict(out=out, pattern=pattern, base=base, channel_multiplier=cm)
        if WHERE[out[1]][0] != "SI":
            kw["allow_small_or_imprecise_dtypes"] = True
        return op("g", "iota", **kw)

    def scan(out, a, b, o1):
        return op("v", "tensor_tensor_scan", out=out, data0=a, data1=b, initial=0.0, op0=A.add, op1=o1)

    def load(q, dst, src, k):
        return rec(q, 0.1, 4.0, [], [dst], lambda e: e.dma_start(res(dst), src), "ld%d" % k, 16)

    def store(dst, srcv, k):
        return rec("y", 0.1, 2.0, [srcv], [], lambda e: e.dma_start(dst, res(srcv)), "st%d" % k, 16)

    def hv(name, c, w=128):
        return v(name, w * c, w * c + w)

    def turn(c):
        if [q for q in PEQ if q // 2 == c]:
            mm(v("b7", 0, 128), hv("z", c), v("Ib"))
            act(hv("zT", c), v("b7", 0, 128), scale=-1.0)

    load("y", v("NBi", 0, 640), T.nbr[:, 0:640], 0)
    load("S", v("z"), T.z0[:], 1)
    load("S", v("NBi", 640, 1280), T.nbr[:, 640:1280], 2)
    load("y", v("KK0", 0, 1280), T.ring[:], 3)
    load("S", v("thI", 0, 1), T.thr[:], 4)
    load("y", v("X"), T.mat[:], 5)

    iota(v("PI"), [[1, 1]], 0, 1)
    iota(v("D2"), [[-16, 8], [0, 16]], 128, 1)
    iota(v("D1"), [[-1, 256]], 256, 1)
    iota(v("iv"), [[80, 16]], 0, 0)
    iota(v("D3"), [[0, 16], [1, 16]], 0, 0)
    iota(v("ic"), [[1, 16]], 0, 0)
    iota(v("V2"), [[10, 256]], 1, 0)
    iota(v("LPh"), [[0, 128]], 0, 16)
    iota(v("LPl"), [[0, 8], [1, 16]], 0, 0)
    iota(v("UC"), [[-256, 256]], 65536, 0)
    iota(v("t1"), [[128, 2], [0, 8]], 1280, 1)
    iota(v("w2"), [[512, 2], [0, 8]], -1280, 4)
    iota(v("T1"), [[1, 1280]], 0, 0)
    ts(v("pi15"), v("PI"), 15, A.bitwise_and)
    cp(v("pcol"), v("pi15"))
    ts(v("p5"), v("pcol"), 5.0, A.mult)
    ts(v("vO", 0, 16), v("iv"), v("p5"), A.add)
    ts(v("pm0"), v("pcol"), -1.0, A.mult, 16.0, A.add)
    ts(v("D2"), v("D2"), 4, A.arith_shift_right)
    ts(v("G16f"), v("D2"), 8.0, A.is_equal)
    ts(v("G16b"), v("D2"), 8.0, A.is_equal)
    cp(v("G8f"), v("G16f", 0, 128, 16))
    cp(v("G8b"), v("G16f", 0, 128, 16))
    ts(v("G8s"), v("G16f", 0, 128, 16), float(WS), A.mult)
    ts(v("G8k"), v("G16f", 0, 128, 16), 4096.0, A.mult)
    ts(v("D15"), v("D1"), 15, A.bitwise_and)
    ts(v("DM"), v("D15"), 0.0, A.is_equal)
    ts(v("RN"), v("D3"), 0.0, A.is_equal, -BIG, A.mult)
    ts(v("RP"), v("RN", 0, 128), -1.0, A.mult)
    ts(v("If"), v("D1", 0, 128), 256.0, A.is_equal)
    ts(v("Ib"), v("D1", 0, 128), 256.0, A.is_equal)
    ts(v("kcol"), v("pcol"), -float(SB), A.mult, -35.0 * SB, A.add)
    cp(v("bl"), v("ic"))
    ts(v("bl2"), v("ic"), 16.0, A.mult, 15.0, A.add)
    for t in range(RO):
        ts(v("pl%d" % t), v("pcol"), 811.0, A.mult, t - 0.375, A.add)
        if t:
            ts(v("pm%d" % t), v("pcol"), -1.0, A.mult, 16.0 + t, A.add)
    ts(v("TriO"), v("D1", 0, 128), 256.0, A.is_lt)
    op("v", "memset", out=v("On"), constant=1.0)
    op("v", "memset", out=v("fb"), constant=-15.0)
    for i in range(2):
        op("v", "memset", out=v("KK%d" % i, 1280, REM), constant=0.0)
    if PEQ:
        for k in range(16):
            cp(v("RS", k, 2048, 16), v("Ib"))
    ts(v("d04"), v("t1"), 8192.0, A.mult)
    ts(v("vmd4"), v("w2"), 8192.0, A.mult)
    ts(v("pb"), v("PI"), 4, A.arith_shift_right, 1, A.bitwise_and)
    cp(v("odd"), v("pb"))
    ts(v("even"), v("odd"), -1.0, A.mult, 1.0, A.add)
    for i in range(4):
        ts(v("pb"), v("PI"), i, A.arith_shift_right, 1, A.bitwise_and)
        f = 2.0 ** -(2 ** i) - 1.0
        if i == 0:
            ts(v("p2"), v("pb"), f, A.mult, 1.0, A.add)
        else:
            ts(v("p2b"), v("pb"), f, A.mult, 1.0, A.add)
            ts(v("p2"), v("p2"), v("p2b"), A.mult)
    ts(v("dcol"), v("p2"), 0.5, A.mult, -0.5, A.add)
    cp(v("thr"), v("thI", 0, 1))
    ts(v("thrc"), v("thr"), float(2 ** 30), A.mult)
    cp(v("B", 0, 640), v("NBi", 0, 640))
    cp(v("B", 640, 1280), v("NBi", 640, 1280))
    for c in range(2):
        cp(v("b1", 128 * c, 128 * c + 128), hv("z", c))
        turn(c)

    def send_rings(t):
        kk = "KK%d" % (t % 2)
        for h in range(2):
            src = v(kk, 512 * h, 512 * h + 512)

            def emit(e, h=h, src=src):
                remote(g, topo, core, rl[h], T["hand%d" % t][:], res(src), T.sem["ha%d" % t], T.sem["ks%d%d" % (t, h)], 8)
            i = rec("g", 0.3, 4.0, [src], [], emit, "ks%d%d" % (t, h), 8)
            lo = REM + 1024 * t + 512 * h
            land(v(kk, lo, lo + 512), "ki%d%d" % (t, h), 8, i)

    def send_revoked(t):
        src = v("rS%d" % t, 0, 1)

        def emit(e):
            remote(g, topo, core, rv_relay, T["hrv%d" % t][:, 0:1], res(src), T.sem["ra%d" % t], T.sem["rs%d" % t], 8)
        i = rec("g", 0.3, 4.0, [src], [], emit, "rs%d" % t, 8)
        land(v("cI%d" % t, 0, 1), "ri%d" % t, 8, i)

    def K(t):
        return v("KK%d" % (t % 2), 0, 1280)

    def vo(t, c):
        b = 16 * (t % 2)
        return v("vO", b + 8 * c, b + 8 * c + 8)

    def first(t, c):
        tab = v("B", 0, 1280) if t else v("NBi")
        bv = hv("Bv", c) if t else v("NBi", 640 * c, 640 * c + 640, 5)
        if t:
            act(bv, ind(tab, vo(t, c)))
        mm(v("b6", 0, 128), v("G16b"), hv("z", c))
        ts(hv("y1", c), v("b6", 0, 128), v("pm%d" % t), A.add)
        ts(hv("y2", c), hv("y1", c), 15, A.bitwise_and)
        oh = v("b1", 256 + 128 * c, 384 + 128 * c)
        ts(oh, hv("y2", c), 0.0, A.is_equal)
        tt(hv("mB", c), oh, bv, A.mult)
        nr = v("b6", 128 + 128 * c, 256 + 128 * c)
        mm(nr, v("G16f"), hv("mB", c))
        mm(v("b6", 384 + 8 * c, 392 + 8 * c), hv("mB", c), v("G8f"))
        tt(hv("dg", c), nr, hv("DM", c), A.mult)
        scan(hv("sc", c), hv("RN", c), hv("dg", c), A.max)
        cp(v("nO", 16 * c, 16 * c + 8), v("sc", 128 * c + 15, 128 * c + 128, 16))
        cp(hv("BnL", c), ind(tab, v("nO", 16 * c, 16 * c + 8)))
        ts(hv("BnC", c), hv("BnL", c), v("kcol"), A.add)
        if t < RO - 1:
            tt(hv("Bk", c), bv, hv("mB", c), A.subtract)

    def second(t, c):
        kv, kn = v("b0", 128 * c, 128 * c + 128), v("b0", 256 + 128 * c, 384 + 128 * c)
        old = K(max(t - 1, 0))
        act(hv("Kv", c), ind(old, vo(t, c)))
        act(hv("Kn", c), ind(old, v("nO", 16 * c, 16 * c + 8)))
        for raw, dst in (("Kv", kv), ("Kn", kn)):
            if raw == "Kv":
                ts(dst, hv(raw, c), 0.0, A.is_equal, -1.0, A.mult)
                tt(dst, dst, hv(raw, c), A.add)
            else:
                ts(dst, hv(raw, c), 0.25, A.max)
            for i, col in ((0, "cI%d" % (t - 2)), (1, "rS%d" % (t - 1))):
                if t - 2 + i >= 0:
                    ts(hv("m%d" % i, c), hv(raw, c), v(col, 0, 1), A.is_equal, -1024.0, A.mult)
                    tt(dst, dst, hv("m%d" % i, c), A.add)
        tt(hv("evn", c), kv, hv("Kn", c), A.is_equal)
        mm(v("b6", 400 + 8 * c, 408 + 8 * c), hv("evn", c), v("G8b"))
        ts(hv("dr", c, 8), v("b6", 400 + 8 * c, 408 + 8 * c), 3.0, A.is_ge, float(DIR), A.mult)
        tt(hv("kn", c, 8), v("b6", 384 + 8 * c, 392 + 8 * c), hv("dr", c, 8), A.add)
        for b in range(128 * c, 128 * c + 128, 32):
            act(v("Kc", 16 * b, 16 * b + 512), ind(old, v("BnL", b, b + 32)))
        for q in (2 * c, 2 * c + 1):
            for eq, b in (("eqV", 0), ("eqN", 256)):
                for k in range(16):
                    s = (1024 * q + k, 1024 * q + 1024, 16)
                    tt(v(eq, *s), v("b0", b + 64 * q, b + 64 * q + 64), v("Kc", *s), A.is_equal)

    def third(t, c):
        for eq, b in (("eqV", "b2"), ("eqN", "b3")):
            mm(v(b, 128 * c, 128 * c + 128), hv("BnC", c), v("If"), True, False)
            for k in range(16):
                mm(v(b, 128 * c + k, 128 * c + 128, 16), v(eq, 2048 * c + k, 2048 * c + 2048, 16), v("G8s"), False, k == 15)
        act(hv("cV", c), v("b2", 128 * c, 128 * c + 128))
        tt(hv("mn", c), v("b3", 128 * c, 128 * c + 128), hv("cV", c), A.min)
        scan(hv("sc2", c), v("RN", 0, 128), hv("mn", c), A.max)
        tt(hv("W", c, 8), v("sc2", 128 * c + 15, 128 * c + 128, 16), hv("kn", c, 8), A.max)
        cp(hv("Wi", c, 8), hv("W", c, 8))
        ts(hv("wT", c, 8), hv("Wi", c, 8), SB - 1, A.bitwise_and)
        tt(hv("Aw", c), ind(hv("wT", c, 8), v("bl", 0, 8)), v("DM", 0, 128), A.mult)
        o = v("b6", 416 + 8 * c, 424 + 8 * c)
        mm(o, hv("Aw", c), v("G8f"))
        w = vo(t + 1, c)
        cp(w, o)
        tt(hv("kp", c), ind(K(t), w), hv("V2", c), A.mult)
        ts(hv("pl", c), hv("kp", c), 0.25, A.mult, v("pl%d" % t), A.add)
        ts(hv("plm", c), hv("pl", c), 2047, A.bitwise_and)
        cp(hv("PL", c), hv("plm", c))
        for q in (2 * c, 2 * c + 1):
            for b in (64 * q, 64 * q + 32):
                act(v("Xc", 16 * b, 16 * b + 512), ind(v("X"), v("PL", b, b + 32)))
            if q in PEQ:
                for b in range(1024 * q, 1024 * q + 1024, 512):
                    mm(v("b7"), v("Ib"), v("Xc", b, b + 512), True, False)
                    mm(v("b7"), hv("zT", c), v("RS", b - 2048 * c, b - 2048 * c + 512), False, True)
                    act(v("ab", b, b + 512), v("b7"), AF.Abs)
                continue
            for k in range(16):
                s = (1024 * q + k, 1024 * q + 1024, 16)
                tt(v("df", *s), v("b1", 64 * q, 64 * q + 64), v("Xc", *s), A.subtract)
            act(v("ab", 1024 * q, 1024 * q + 1024), v("df", 1024 * q, 1024 * q + 1024), AF.Abs)
        act(hv("Kw", c), ind(K(t), w))
        ts(hv("hz", c), hv("Kw", c), 0.0, A.is_equal, float(2 ** 25), A.mult)
        if t < RO - 1:
            act(hv("Vn", c), ind(v("T1"), w))
            act(hv("V2", c), hv("Vn", c), scale=2.0, bias=1.0)
        tt(hv("pr", c), v("b1", 128 * c, 128 * c + 128), hv("Kw", c), A.mult)
        mm(v("b6", 448 + 8 * c, 456 + 8 * c), hv("pr", c), v("G8f"))
        pa = v("b5", 256 + 128 * c, 384 + 128 * c)
        mm(pa, v("Ib"), hv("Kw", c), True, False)
        mm(pa, v("Ib"), hv("UC", c), False, True)

    def fourth(t, c):
        dT = v("b4", 128 * c, 128 * c + 128)
        mm(dT, v("Ib"), v("LPh"), True, False)
        mm(dT, v("Ib"), v("LPl"), False, False)
        for p in range(16):
            mm(v("b4", 128 * c + p, 128 * c + 128, 16), v("ab", 2048 * c + p, 2048 * c + 2048, 16), v("G8k"), False, p == 15)
        act(hv("dk", c), dT)
        scan(hv("sd", c), v("RP"), dT, A.min)
        mm(v("b5", 128 * c, 128 * c + 128), v("Ib"), hv("hz", c), True, False)
        mm(v("b5", 128 * c, 128 * c + 128), hv("dk", c), v("If"), False, True)
        tt(hv("Ap", c), ind(hv("sd", c), v("bl2", 0, 8)), v("DM", 0, 128), A.mult)
        o = v("b6", 432 + 8 * c, 440 + 8 * c)
        mm(o, hv("Ap", c), v("G8f"))
        cp(hv("pi", c, 8), o)
        ts(hv("pi2", c, 8), hv("pi", c, 8), 2047, A.bitwise_and)
        do = v("dO", 16 * c, 16 * c + 8)
        cp(do, hv("pi2", c, 8))
        tt(hv("zx", c), ind(v("Xc", 2048 * c, 2048 * c + 2048), do), hv("z", c), A.add)
        ts(hv("dz", c), hv("zx", c), 0.5, A.mult, -0.25, A.add)
        zp = v("b1", 128 * c, 128 * c + 128)
        if t == RO - 1:
            cp(hv("zF", c), hv("dz", c))
            store(T.yz[:, 128 * c:128 * c + 128], hv("zF", c), c)
        else:
            cp(hv("z", c), hv("dz", c))
            cp(zp, hv("z", c))
            turn(c)
        act(hv("cd", c), v("b5", 128 * c, 128 * c + 128), AF.Relu, scale=-float(2 ** 18), bias=v("thrc"))
        tt(hv("rr", c), v("b5", 256 + 128 * c, 384 + 128 * c), hv("cd", c), A.min)

    def writers(t):
        ts(v("F"), v("W"), float(SB), A.is_lt)
        ts(v("NF"), v("W"), float(SB), A.is_ge, -512.0, A.mult)
        ts(v("Lb"), v("W"), float(DIR), A.is_lt)
        mm(v("b2", 400, 408), v("TriO"), v("F", 0, 8), True, False)
        mm(v("b2", 400, 408), v("Ib"), v("NF", 0, 8), False, True)
        mm(v("b2", 408, 416), v("TriO"), v("F", 8, 16), True, False)
        mm(v("b2", 408, 416), v("Ib"), v("NF", 8, 16), False, False)
        mm(v("b2", 408, 416), v("On"), v("F", 0, 8), False, True)
        ts(v("x96"), v("b2", 400, 416), float(CAP), A.is_lt)
        tt(v("act"), v("x96"), v("Lb"), A.mult)
        tt(v("av"), v("act"), v("vmd4"), A.mult)
        cp(v("hi"), v("b6", 448, 464))
        ts(v("h2"), v("hi"), 1023, A.bitwise_and)
        ts(v("hb"), v("h2"), float(REM + 1024 * t), A.add)
        tt(v("hc"), v("hb"), v("F"), A.mult)
        tt(v("src"), v("hc"), v("wT"), A.max)
        tt(v("hd"), v("src"), v("d04"), A.add)
        w2 = v("av")
        if t:
            for gr in range(8):
                e, f = 256 * gr, 128 * gr
                mm(v("b2", 416 + gr, 417 + gr), v("EA", e, e + 128), v("act", gr, gr + 1))
                mm(v("b2", 424 + gr, 425 + gr), v("EA", e + 128, e + 256), v("act", gr, gr + 1), True, False)
                mm(v("b2", 424 + gr, 425 + gr), v("EB", f, f + 128), v("act", 8 + gr, 9 + gr), False, True)
            ts(v("wr"), v("b2", 416, 432), 0.0, A.is_equal)
            tt(v("w2"), v("wr"), v("av"), A.mult)
            w2 = v("w2")
        tt(v("word"), w2, v("hd"), A.add)
        tt(v("Aq"), ind(v("word"), v("bl")), v("DM"), A.mult)
        for c in range(2):
            mm(v("b2", 448 + 8 * c, 456 + 8 * c), hv("Aq", c), v("G8f"))
        cp(v("qi"), v("b2", 448, 464))
        ts(v("q1"), v("qi"), 13, A.arith_shift_right)
        cp(v("scO"), v("q1"))
        ts(v("q2"), v("qi"), 8191, A.bitwise_and)
        cp(v("srO"), v("q2"))
        act(v("sgn"), v("b0", 0, 256), AF.Sign)
        act(v("hole"), v("sgn"), AF.Relu, scale=-1.0)
        act(v("Kvr"), v("b0", 0, 256), AF.Relu)
        kk = "KK%d" % (t % 2)
        tt(v("fm"), ind(v(kk, 0, REM + 1024 * (t + 1)), v("srO")), v("hole"), A.mult)
        tt(ind(v(kk, 0, REM), v("scO")), v("fm"), v("Kvr"), A.add)
        if t < RO - 1:
            tt(v("ohw"), v("b1", 256, 512), v("Vn"), A.mult)
            tt(ind(v("B"), v("scO")), v("Bk"), v("ohw"), A.add)
            mm(v("b2", 432, 448), v("On"), v("F"))
            act(v("fj"), v("b2", 432, 448), accum_out=v("fs"))
            cp(v("fi"), v("fs"))
            ts(v("fa"), v("fi"), 15, A.bitwise_and)
            ts(v("t1"), v("wT"), 8192.0, A.mult)
            tt(v("vmd4"), v("t1"), v("d04"), A.subtract)

    def same_node():
        ts(v("ci"), v("Vn"), v("p2"), A.mult, v("dcol"), A.add)
        ts(v("cb"), v("ci"), 1, A.bitwise_and)
        ts(v("code"), v("cb"), -2.0, A.mult, 1.0, A.add)
        act(v("cdE"), v("code"), scale=v("even"))
        act(v("cdO"), v("code"), scale=v("odd"))
        for gr in range(8):
            lo = 32 * (gr // 2)
            m = "cdO" if gr % 2 else "cdE"
            b = "b3" if gr % 2 else "b7"
            mm(v(b, 0, 256), v(m, 0, 128, 1, lo, lo + 32), v("code", 0, 256, 1, lo, lo + 32))
            mm(v(b, 256, 384), v(m, 128, 256, 1, lo, lo + 32), v("code", 128, 256, 1, lo, lo + 32))
            act(v("E0", 256 * gr, 256 * gr + 256), v(b, 0, 256), AF.Relu, bias=v("fb"))
            act(v("E1", 128 * gr, 128 * gr + 128), v(b, 256, 384), AF.Relu, bias=v("fb"))
        for e, o, w in (("E0", "EA", 256), ("E1", "EB", 128)):
            op("g", "affine_select", out=v(o), in_=v(e), pattern=[[0, 8], [1, w]], compare_op=A.is_gt, fill=0.0, base=0,
               channel_multiplier=-1)

    def revoke(t):
        if t:
            come = v("cI%d" % (t - 1), 0, 1)
            ts(v("ncome"), come, -1.0, A.mult)
            ts(v("NM2"), K(t), come, A.is_equal, v("ncome"), A.mult)
        op("v", "tensor_reduce", out=v("rvi"), in_=v("rr"), axis=AxisListType.X, op=A.max)
        ts(v("rva"), v("rvi"), 255, A.bitwise_and)
        rv = v("rS%d" % t, 0, 1)
        cp(rv, v("rva"))
        if t:
            ts(v("rvE%d" % t), rv, v("cI%d" % (t - 1), 0, 1), A.not_equal, rv, A.mult)
            rv = v("rvE%d" % t)
        ts(v("nrv"), rv, -1.0, A.mult)
        kk = "KK%d" % (t % 2)
        blocks = ((0, 512, "b4"), (512, 1024, "b7"), (1024, 1280, "b4"))
        for lo, hi, b in blocks:
            ts(v("NM1", lo, hi), v(kk, lo, hi), rv, A.is_equal, v("nrv"), A.mult)
        for lo, hi, b in blocks:
            o = v(b, 0, hi - lo)
            mm(o, v("Ib"), v(kk, lo, hi), True, False)
            if t:
                mm(o, v("Ib"), v("NM2", lo, hi), False, False)
            mm(o, v("Ib"), v("NM1", lo, hi), False, True)
            if t == RO - 1:
                act(v("Yk", lo, hi), o)
                store(T.yk[:, lo:hi], v("Yk", lo, hi), 2 + lo // 512)
            else:
                act(v("KK%d" % ((t + 1) % 2), lo, hi), o)
        if t < RO - 1:
            send_revoked(t)
            send_rings(t + 1)
            ts(v("thrc"), v("fa"), v("thr"), A.add, float(2 ** 30), A.mult)

    send_rings(0)
    for c in range(2):
        first(0, c)
    for t in range(RO):
        for c in range(2):
            second(t, c)
        for c in range(2):
            third(t, c)
        writers(t)
        fourth(t, 0)
        if t < RO - 1:
            first(t + 1, 0)
        fourth(t, 1)
        revoke(t)
        if t < RO - 1:
            first(t + 1, 1)
            same_node()
    if not SEQ:
        SEQ.append(order(ops))
    issue(g, T, ops, SEQ[0])


def hand_on(g, core, T, topo):
    n = len(T.cores)
    for r in range(n):
        src, below, above = T.cores[r], T.cores[(r - 1) % n], T.cores[(r + 1) % n]
        rl = relays(src, T, topo, below)
        rv_relay = relays(src, T, topo, above)[0]
        if core not in rl and core != rv_relay:
            continue
        for t in range(RO):
            if t and core == rv_relay:
                g.wait_ge(T.sem["ra%d" % (t - 1)], 8)
                remote(g, topo, core, above, T["cI%d" % (t - 1)][:, 0:1], T["hrv%d" % (t - 1)][:, 0:1],
                       T.sem["ri%d" % (t - 1)], T.sem["rl%d" % (t - 1)], 8)
            if core in rl:
                h = rl.index(core)
                g.wait_ge(T.sem["ha%d" % t], 8)
                lo = REM + 1024 * t + 512 * h
                remote(g, topo, core, below, T["KK%d" % (t % 2)][:, lo:lo + 512], T["hand%d" % t][:],
                       T.sem["ki%d%d" % (t, h)], T.sem["hs%d" % t], 8)
        for t in range(RO):
            if core in rl:
                g.wait_ge(T.sem["hs%d" % t], 8)
            if t and core == rv_relay:
                g.wait_ge(T.sem["rl%d" % (t - 1)], 8)
